import numpy as np
import ml_dtypes


def mxq(x, axis, fmt="e4m3"):
    dtype, down = {"e4m3": (ml_dtypes.float8_e4m3fn, 7), "e5m2": (ml_dtypes.float8_e5m2, 14)}[fmt]
    v = np.moveaxis(np.asarray(x, np.float32).astype(ml_dtypes.bfloat16).astype(np.float64), axis, -1)
    blocks = v.reshape(v.shape[:-1] + (-1, 32))
    amax = np.abs(blocks).max(-1, keepdims=True)
    byte = np.maximum(np.where(amax > 0, np.frexp(amax)[1] - 1 + 127, 0) - down, 1)
    scale = np.exp2(byte - 127.0)
    codes = (blocks / scale).astype(np.float32).astype(dtype).astype(np.float64)
    return np.moveaxis((codes * scale).reshape(v.shape), -1, axis)


WIDE = False


def mx_kscale(k):
    if not WIDE:
        return np.ones(k)
    levels = np.array([10, -10, 5, -5, 0])
    if k % 512:
        return np.exp2(np.random.permutation(np.resize(levels, k // 32))).repeat(32)
    a = np.empty((k // 512, 16))
    for p in range(k // 512):
        a[p, :8] = np.random.permutation(np.resize(levels, 8))
        for g in range(8):
            far = levels[np.abs(levels - a[p, g]) >= 10]
            a[p, g + 8] = far[np.random.randint(len(far))]
    return np.exp2(a.ravel()).repeat(32)


def f64(x):
    return np.asarray(x).astype(np.float64)


def striped(idx):
    return np.tile(idx.reshape(-1, 16).T, (8, 1)).astype(np.uint16)


def unstriped(offs):
    return offs[:16].T.reshape(-1).astype(np.int64)


def striped8(idx):
    return np.concatenate([x.reshape(-1, 16).T for x in idx]).astype(np.uint16)


def runs(offs, k):
    lists = np.stack([offs[16 * r : 16 * r + 16].T.reshape(-1) for r in range(8)]).astype(np.int64)
    return lists[np.arange(k) % 512 // 64]


def pack_weight(w):
    k, n = w.shape
    w = f64(np.asarray(w, np.float32).astype(ml_dtypes.bfloat16)).reshape(k // 32, 32, n)
    amax = np.abs(w).max(1)
    byte = np.clip(np.where(amax > 0, np.frexp(amax)[1] - 1 + 127 - 7, 1), 1, 254)
    scaled = (w * np.exp2(127.0 - byte)[:, None, :]).reshape(k, n).astype(np.float32)
    words = np.ascontiguousarray(scaled.reshape(k // 512, 128, 4, n).transpose(0, 1, 3, 2)).astype(ml_dtypes.float8_e4m3fn).view(np.uint8)
    return words, np.ascontiguousarray(byte.astype(np.uint8).reshape(k // 512, 16, n))


def unpack_weight(words, scales):
    g, p, n, _ = words.shape
    vals = np.ascontiguousarray(words).view(ml_dtypes.float8_e4m3fn).astype(np.float64) * np.repeat(np.exp2(scales.astype(np.float64) - 127.0), 8, axis=1)[..., None]
    return vals.transpose(0, 1, 3, 2).reshape(g * 512, n)


E2M1 = np.array([0.0, 0.5, 1.0, 1.5, 2.0, 3.0, 4.0, 6.0, -0.0, -0.5, -1.0, -1.5, -2.0, -3.0, -4.0, -6.0])


def pack_fp4(w):
    k, n = w.shape
    w = f64(np.asarray(w, np.float32).astype(ml_dtypes.bfloat16)).reshape(k // 32, 32, n)
    amax = np.abs(w).max(1)
    mant, ex = np.frexp(amax / 6.0)
    byte = np.clip(np.where(amax > 0, np.where(mant > 0.5, ex, ex - 1) + 127, 1), 1, 254)
    scaled = (w * np.exp2(127.0 - byte)[:, None, :]).reshape(k, n).astype(np.float32)
    c = np.ascontiguousarray(scaled.reshape(k // 512, 128, 4, n).transpose(0, 1, 3, 2)).astype(ml_dtypes.float4_e2m1fn).view(np.uint8) & 0xF
    words = (c[..., 0::2] | (c[..., 1::2] << 4)).reshape(k // 512, 128, 2 * n)
    return np.ascontiguousarray(words), np.ascontiguousarray(byte.astype(np.uint8).reshape(k // 512, 16, n))


def unpack_fp4(words, scales):
    g, _, n = scales.shape
    words = np.ascontiguousarray(words).reshape(g, 128, n, 2)
    nib = np.empty((g, 128, n, 4), np.uint8)
    nib[..., 0::2] = words & 0xF
    nib[..., 1::2] = words >> 4
    vals = E2M1[nib] * np.repeat(np.exp2(scales.astype(np.float64) - 127.0), 8, axis=1)[..., None]
    return vals.transpose(0, 1, 3, 2).reshape(g * 512, n)


def planes(y):
    n, m = y.shape
    v = y.astype(np.float32).astype(ml_dtypes.bfloat16).astype(np.float64).reshape(n // 32, 32, m)
    top = np.abs(v).max(1)
    byte = np.clip(np.where(top > 0, np.frexp(top)[1] - 1 + 127 - 7, 1), 1, 254)
    codes = (v * np.exp2(127.0 - byte)[:, None, :]).reshape(n, m).astype(np.float32).astype(ml_dtypes.float8_e4m3fn).view(np.uint8)
    words = codes.reshape(n // 512, 128, 4, m).transpose(0, 1, 3, 2)
    return np.ascontiguousarray(words), np.ascontiguousarray(byte.astype(np.uint8).reshape(n // 512, 16, m))


K, T, S, N, H = 512, 2048, 512, 512, 512


def setup_inputs():
    n = np.random.standard_normal
    s = mx_kscale(K)[:, None]
    u = mx_kscale(H)
    packed_xT = pack_weight(n((K, T)) * s)
    packed_w1 = pack_fp4(n((K, H)) / np.sqrt(K) / s)
    packed_w2 = pack_fp4(n((H, N)) / np.sqrt(H) / u[:, None])
    packed_w3 = pack_fp4(n((H, N)) / np.sqrt(H) / u[:, None])
    return {
        "x_words": packed_xT[0],
        "x_scales": packed_xT[1],
        "w1_words": packed_w1[0],
        "w1_scales": packed_w1[1],
        "gn": (np.random.uniform(0.5, 1.5, (H, 1)) * u[:, None]).astype(np.float32),
        "w2_words": packed_w2[0],
        "w2_scales": packed_w2[1],
        "gm": (np.random.uniform(0.5, 1.5, (H, 1)) * u[:, None]).astype(np.float32),
        "w3_words": packed_w3[0],
        "w3_scales": packed_w3[1],
        "offs": striped(np.random.permutation(T)[:S]),
        "n1": striped8(np.stack([np.random.permutation(S) for _ in range(8)])),
        "n2": striped8(np.stack([np.random.permutation(S) for _ in range(8)])),
        "n3": striped8(np.stack([np.random.permutation(S) for _ in range(8)])),
        "n4": striped8(np.stack([np.random.permutation(S) for _ in range(8)])),
        "n5": striped8(np.stack([np.random.permutation(S) for _ in range(8)])),
        "n6": striped8(np.stack([np.random.permutation(S) for _ in range(8)])),
    }


def reference(x_words, x_scales, w1_words, w1_scales, gn, w2_words, w2_scales, gm, w3_words, w3_scales, offs, n1, n2, n3, n4, n5, n6):
    xq = unpack_weight(x_words, x_scales)[:, unstriped(offs)]
    y = unpack_fp4(w1_words, w1_scales).T @ xq
    z = f64(gn) * ((y - (y[np.arange(H)[:, None], runs(n1, H)])) / (np.abs(y[np.arange(H)[:, None], runs(n2, H)] - y) + 0.5))
    a = unpack_fp4(w2_words, w2_scales).T @ mxq(z, 0, "e4m3")
    z2 = f64(gm) * (y * (y[np.arange(H)[:, None], runs(n3, H)] - (y[np.arange(H)[:, None], runs(n4, H)])))
    b = unpack_fp4(w3_words, w3_scales).T @ mxq(z2, 0, "e4m3")
    out_0 = np.maximum(a, b[np.arange(N)[:, None], runs(n6, N)]) - (np.minimum(a[np.arange(N)[:, None], runs(n5, N)], b))
    return (out_0,) + planes(out_0)

@@ -1,0 +1,239 @@
+from contextlib import ExitStack
+
+import concourse.mybir as mybir
+
+K, T, S, N, H = 512, 2048, 512, 512, 512
+FLOPS = 2 * K * H * S + 2 * 2 * H * N * S
+
+F32 = mybir.dt.float32
+BF16 = mybir.dt.bfloat16
+I32 = mybir.dt.int32
+U32 = mybir.dt.uint32
+U16 = mybir.dt.uint16
+U8 = mybir.dt.uint8
+FP8X4 = mybir.dt.float8_e4m3fn_x4
+FP4X4 = mybir.dt.float4_e2m1fn_x4
+ALU = mybir.AluOpType
+ACT = mybir.ActivationFunctionType
+
+P = 128
+PACK = 4
+HALF = S // 2
+
+
+def load_scale_rows(queue, plane, scales):
+    for q in range(4):
+        queue.dma_start(out=plane[32 * q : 32 * q + 4, :].bitcast(I32), in_=scales[0, 4 * q : 4 * q + 4, :].bitcast(I32))
+
+
+def deal(nc, words, plane, raw_words, raw_plane):
+    nc.vector.tensor_copy(
+        out=words.rearrange("p (t m b) -> p t m b", t=PACK, b=2),
+        in_=raw_words.rearrange("p (m t b) -> p t m b", t=PACK, b=2),
+    )
+    nc.vector.tensor_copy(
+        out=plane.rearrange("p (t m) -> p t m", t=PACK),
+        in_=raw_plane.rearrange("p (m t) -> p t m", t=PACK),
+    )
+
+
+def product(nc, bank, words, plane, t, codes, scales):
+    nc.tensor.matmul_mx(
+        out=bank,
+        lhsT=words[:, 2 * P * t : 2 * P * (t + 1)].bitcast(FP4X4),
+        lhsT_scale=plane[:, P * t : P * (t + 1)],
+        rhs=codes.bitcast(FP8X4),
+        rhs_scale=scales,
+        start=True,
+        stop=True,
+    )
+
+
+def interleave(nc, grouped, planes, scale):
+    nc.scalar.activation(
+        out=grouped.rearrange("p (c i t) -> p c t i", i=4, t=PACK),
+        in_=planes.rearrange("p t (c i) -> p c t i", i=4),
+        func=ACT.Copy,
+        scale=scale,
+    )
+
+
+def tile_picked_forkmaxbfracwind_none_po_kernel(
+    tc, x_words, x_scales, w1_words, w1_scales, gn, w2_words, w2_scales, gm, w3_words, w3_scales,
+    offs, n1, n2, n3, n4, n5, n6, out_0, out_1, out_2,
+):
+    nc = tc.nc
+    with ExitStack() as ctx:
+        keep = ctx.enter_context(tc.tile_pool(name="keep", bufs=1))
+        psum = ctx.enter_context(tc.psum_pool(name="psum", bufs=1))
+
+        def sb(name, shape, dtype):
+            return keep.tile(shape, dtype, name=name, align_bytes=64)
+
+        lists = {}
+        for name in ("offs", "n1", "n2", "n3", "n4", "n5", "n6"):
+            lists[name] = keep.tile([P, S // 16], U16, name="list_" + name)
+
+        x_plane = sb("x_plane", [P, T], U8)
+        raw_planes = sb("raw_planes", [P, 3, H], U8)
+        nc.vector.memset(x_plane[:].bitcast(I32), 0)
+        nc.vector.memset(raw_planes[:].rearrange("p w n -> p (w n)").bitcast(I32), 0)
+
+        four = sb("four", [P, 1], F32)
+        half = sb("half", [P, 1], F32)
+        nc.vector.memset(four[:], 4.0)
+        nc.scalar.activation(out=half[:], in_=four[:], func=ACT.Abs_reciprocal_sqrt)
+
+        raw_words = [sb("raw_words%d" % w, [P, 2 * H], U8) for w in range(3)]
+        x_table = sb("x_table", [P, T], U32)
+        nc.sync.dma_start(lists["offs"][:], offs)
+        nc.sync.dma_start(out=raw_words[0][:].bitcast(I32), in_=w1_words[0].bitcast(I32))
+        load_scale_rows(nc.sync, x_plane, x_scales)
+        load_scale_rows(nc.gpsimd, raw_planes[:, 0, :], w1_scales)
+        nc.sync.dma_start(out=x_table[:].bitcast(I32), in_=x_words[0].rearrange("p n t -> p (n t)").bitcast(I32))
+        nc.sync.dma_start(lists["n4"][:], n4)
+        nc.sync.dma_start(lists["n2"][:], n2)
+        nc.sync.dma_start(lists["n3"][:], n3)
+        gains_m = sb("gains_m", [P, PACK], F32)
+        gains_n = sb("gains_n", [P, PACK], F32)
+        nc.sync.dma_start(out=raw_words[2][:].bitcast(I32), in_=w3_words[0].bitcast(I32))
+        load_scale_rows(nc.sync, raw_planes[:, 2, :], w3_scales)
+        nc.sync.dma_start(out=raw_words[1][:].bitcast(I32), in_=w2_words[0].bitcast(I32))
+        load_scale_rows(nc.sync, raw_planes[:, 1, :], w2_scales)
+        nc.sync.dma_start(out=gains_m[:], in_=gm.rearrange("(p t) o -> p (t o)", t=PACK))
+        nc.sync.dma_start(out=gains_n[:], in_=gn.rearrange("(p t) o -> p (t o)", t=PACK))
+        nc.sync.dma_start(lists["n1"][:], n1)
+        nc.sync.dma_start(lists["n6"][:], n6)
+        nc.sync.dma_start(lists["n5"][:], n5)
+
+        y_win = [sb("y_win%d" % t, [P, 2 * S], F32) for t in range(PACK)]
+        y_last = sb("y_last", [P, S], F32)
+        nc.gpsimd.memset(y_win[0][:, S:], 0.0)
+        y_plain = [y_win[t + 1][:, S:] for t in range(PACK - 1)] + [y_last[:]]
+
+        w_words = [sb("w_words%d" % w, [P, 2 * H], U8) for w in range(3)]
+        w_plane = [sb("w_plane%d" % w, [P, H], U8) for w in range(3)]
+        deal(nc, w_words[0][:], w_plane[0][:], raw_words[0][:], raw_planes[:, 0, :])
+
+        xq_scales = sb("xq_scales", [P, S], U8)
+        xq_codes = sb("xq_codes", [P, S], U32)
+        nc.vector.tensor_copy(xq_scales[:], x_plane[:].indirect(lists["offs"][:]))
+        nc.vector.tensor_copy(xq_codes[:], x_table[:].indirect(lists["offs"][:]))
+
+        y_bank = [psum.tile([P, S], F32, name="y_bank%d" % t, tag="low%d" % t) for t in range(PACK)]
+        for t in range(PACK):
+            product(nc, y_bank[t][:], w_words[0], w_plane[0], t, xq_codes[:], xq_scales[:])
+        deal(nc, w_words[2][:], w_plane[2][:], raw_words[2][:], raw_planes[:, 2, :])
+        deal(nc, w_words[1][:], w_plane[1][:], raw_words[1][:], raw_planes[:, 1, :])
+
+        y4 = [sb("y4_%d" % t, [P, S], F32) for t in range(PACK)]
+        d34 = [sb("d34_%d" % t, [P, S], F32) for t in range(PACK)]
+        d2 = [sb("d2_%d" % t, [P, S], F32) for t in range(PACK)]
+        d1 = [sb("d1_%d" % t, [P, S], F32) for t in range(PACK)]
+        dist = [sb("dist_%d" % t, [P, S], F32) for t in range(PACK)]
+        den2 = [sb("den2_%d" % t, [P, S], F32) for t in range(PACK)]
+        inv = [sb("inv_%d" % t, [P, S], F32) for t in range(PACK)]
+        z2 = sb("z2", [P, PACK, S], F32)
+        z = sb("z", [P, PACK, S], F32)
+
+        def z2_plane(t):
+            nc.vector.scalar_tensor_tensor(
+                out=z2[:, t, :], in0=d34[t][:], scalar=gains_m[:, t : t + 1], in1=y_plain[t], op0=ALU.mult, op1=ALU.mult
+            )
+
+        def z_plane(t):
+            nc.vector.scalar_tensor_tensor(
+                out=z[:, t, :], in0=d1[t][:], scalar=gains_n[:, t : t + 1], in1=inv[t][:], op0=ALU.mult, op1=ALU.mult
+            )
+
+        for t in range(PACK):
+            nc.scalar.copy(out=y_win[t][:, :S], in_=y_bank[t][:])
+            nc.scalar.copy(out=y_plain[t], in_=y_bank[t][:])
+        for t in range(PACK):
+            nc.vector.tensor_copy(y4[t][:], y_win[t][:].indirect(lists["n4"][:]))
+            if t > 0:
+                z2_plane(t - 1)
+            nc.vector.tensor_tensor(d2[t][:], y_win[t][:].indirect(lists["n2"][:]), y_plain[t], ALU.subtract)
+            nc.vector.tensor_tensor(d34[t][:], y_win[t][:].indirect(lists["n3"][:]), y4[t][:], ALU.subtract)
+            nc.scalar.activation(out=dist[t][:], in_=d2[t][:], func=ACT.Abs)
+            nc.scalar.activation(out=den2[t][:], in_=dist[t][:], func=ACT.Square, bias=half[:])
+            nc.scalar.activation(out=inv[t][:], in_=den2[t][:], func=ACT.Abs_reciprocal_sqrt)
+
+        def first_gather(t):
+            nc.vector.tensor_tensor(d1[t][:], y_win[t][:].indirect(lists["n1"][:]), y_plain[t], ALU.subtract)
+
+        first_gather(0)
+        z2_plane(PACK - 1)
+        z2_bf = sb("z2_bf", [P, PACK * S], BF16)
+        interleave(nc, z2_bf[:], z2[:], 1.0)
+        first_gather(1)
+        z_plane(0)
+        first_gather(2)
+        z2_codes = sb("z2_codes", [P, S], U32)
+        z2_scales = sb("z2_scales", [P, S], U8)
+        nc.vector.quantize_mx(out=z2_codes[:].bitcast(FP8X4), scales=z2_scales[:], in_=z2_bf[:])
+        b_bank = [psum.tile([P, S], F32, name="b_bank%d" % t, tag="high%d" % t) for t in range(PACK)]
+        b_win = [sb("b_win%d" % t, [P, S], F32) for t in range(PACK)]
+        for t in range(PACK):
+            product(nc, b_bank[t][:], w_words[2], w_plane[2], t, z2_codes[:], z2_scales[:])
+            nc.scalar.copy(out=b_win[t][:], in_=b_bank[t][:])
+        z_plane(1)
+        first_gather(3)
+        z_plane(2)
+        z_plane(3)
+        z_bf = sb("z_bf", [P, PACK * S], BF16)
+        interleave(nc, z_bf[:], z[:], -1.0)
+
+        b6 = [sb("b6_%d" % t, [P, S], F32) for t in range(PACK)]
+
+        def cols(h):
+            return slice(h * HALF, (h + 1) * HALF)
+
+        def entries(name, h):
+            return lists[name][:, h * HALF // 16 : (h + 1) * HALF // 16]
+
+        def b_gather(t):
+            for h in range(2):
+                nc.vector.tensor_copy(b6[t][:, cols(h)], b_win[t][:].indirect(entries("n6", h)))
+
+        b_gather(0)
+        b_gather(1)
+        z_codes = sb("z_codes", [P, S], U32)
+        z_scales = sb("z_scales", [P, S], U8)
+        nc.vector.quantize_mx(out=z_codes[:].bitcast(FP8X4), scales=z_scales[:], in_=z_bf[:])
+        a_bank = [psum.tile([P, S], F32, name="a_bank%d" % t, tag="low%d" % t) for t in range(PACK)]
+        a_win = [sb("a_win%d" % t, [P, S], F32) for t in range(PACK)]
+        for t in range(PACK):
+            product(nc, a_bank[t][:], w_words[1], w_plane[1], t, z_codes[:], z_scales[:])
+            nc.scalar.copy(out=a_win[t][:], in_=a_bank[t][:])
+        b_gather(2)
+        b_gather(3)
+
+        larger = [sb("larger%d" % t, [P, S], F32) for t in range(PACK)]
+        out_codes = sb("out_codes", [P, S], U32)
+        out_scales = sb("out_scales", [P, S], U8)
+        out_rows = out_0.rearrange("(p t) j -> p t j", t=PACK)
+        out_words = out_1[0].rearrange("p n t -> p (n t)").bitcast(I32)
+        for h in range(2):
+            a5 = [sb("a5_%d_%d" % (h, t), [P, HALF], F32) for t in range(PACK)]
+            smaller = [sb("smaller%d_%d" % (h, t), [P, HALF], F32) for t in range(PACK)]
+            result = sb("result%d" % h, [P, PACK, HALF], F32)
+            for step in range(PACK + 2):
+                if step < PACK:
+                    nc.vector.tensor_copy(a5[step][:], a_win[step][:].indirect(entries("n5", h)))
+                    if h == 0:
+                        nc.vector.tensor_tensor(larger[step][:], b6[step][:], a_bank[step][:], ALU.max)
+                if 1 <= step <= PACK:
+                    t = step - 1
+                    nc.vector.tensor_tensor(smaller[t][:], a5[t][:], b_bank[t][:, cols(h)], ALU.min)
+                if step >= 2:
+                    t = step - 2
+                    nc.vector.tensor_tensor(result[:, t, :], larger[t][:, cols(h)], smaller[t][:], ALU.subtract)
+                    nc.sync.dma_start(out=out_rows[:, t, cols(h)], in_=result[:, t, :])
+            result_bf = sb("result_bf%d" % h, [P, PACK * HALF], BF16)
+            interleave(nc, result_bf[:], result[:], 1.0)
+            nc.vector.quantize_mx(out=out_codes[:, cols(h)].bitcast(FP8X4), scales=out_scales[:, cols(h)], in_=result_bf[:])
+            nc.sync.dma_start(out=out_words[:, cols(h)], in_=out_codes[:, cols(h)].bitcast(I32))
+        for q in range(4):
+            queue = nc.sync if q % 2 == 0 else nc.scalar
+            queue.dma_start(out=out_2[0, 4 * q : 4 * q + 4, :].bitcast(I32), in_=out_scales[32 * q : 32 * q + 4, :].bitcast(I32))

@@ -21,16 +21,19 @@ PACK = 4
 HALF = S // 2
 
 
-def load_scale_rows(queue, plane, scales):
+def load_scale_rows(queues, plane, scales):
     for q in range(4):
-        queue.dma_start(out=plane[32 * q : 32 * q + 4, :].bitcast(I32), in_=scales[0, 4 * q : 4 * q + 4, :].bitcast(I32))
+        queues[q].dma_start(out=plane[32 * q : 32 * q + 4, :].bitcast(I32), in_=scales[0, 4 * q : 4 * q + 4, :].bitcast(I32))
 
 
-def deal(nc, words, plane, raw_words, raw_plane):
+def deal_words(nc, words, raw_words):
     nc.vector.tensor_copy(
         out=words.rearrange("p (t m b) -> p t m b", t=PACK, b=2),
         in_=raw_words.rearrange("p (m t b) -> p t m b", t=PACK, b=2),
     )
+
+
+def deal_plane(nc, plane, raw_plane):
     nc.vector.tensor_copy(
         out=plane.rearrange("p (t m) -> p t m", t=PACK),
         in_=raw_plane.rearrange("p (m t) -> p t m", t=PACK),
@@ -67,8 +70,8 @@ def tile_picked_forkmaxbfracwind_none_po_kernel(
         keep = ctx.enter_context(tc.tile_pool(name="keep", bufs=1))
         psum = ctx.enter_context(tc.psum_pool(name="psum", bufs=1))
 
-        def sb(name, shape, dtype):
-            return keep.tile(shape, dtype, name=name, align_bytes=64)
+        def sb(name, shape, dtype, tag=None):
+            return keep.tile(shape, dtype, name=name, align_bytes=64, tag=tag or name)
 
         lists = {}
         for name in ("offs", "n1", "n2", "n3", "n4", "n5", "n6"):
@@ -76,35 +79,35 @@ def tile_picked_forkmaxbfracwind_none_po_kernel(
 
         x_plane = sb("x_plane", [P, T], U8)
         raw_planes = sb("raw_planes", [P, 3, H], U8)
-        nc.vector.memset(x_plane[:].bitcast(I32), 0)
+        nc.gpsimd.memset(x_plane[:].bitcast(I32), 0)
         nc.vector.memset(raw_planes[:].rearrange("p w n -> p (w n)").bitcast(I32), 0)
+
+        raw_words = [sb("raw_words%d" % w, [P, 2 * H], U8) for w in range(3)]
+        x_table = sb("x_table", [P, T], U32)
+        gains_m = sb("gains_m", [P, PACK], F32)
+        gains_n = sb("gains_n", [P, PACK], F32)
+        nc.sync.dma_start(lists["offs"][:], offs)
+        nc.sync.dma_start(out=raw_words[0][:].bitcast(I32), in_=w1_words[0].bitcast(I32))
+        load_scale_rows([nc.sync] * 4, x_plane, x_scales)
+        nc.sync.dma_start(out=x_table[:].bitcast(I32), in_=x_words[0].rearrange("p n t -> p (n t)").bitcast(I32))
+        load_scale_rows([nc.sync] * 4, raw_planes[:, 0, :], w1_scales)
+        nc.sync.dma_start(out=raw_words[2][:].bitcast(I32), in_=w3_words[0].bitcast(I32))
+        nc.sync.dma_start(out=raw_words[1][:].bitcast(I32), in_=w2_words[0].bitcast(I32))
+        nc.sync.dma_start(lists["n4"][:], n4)
+        nc.sync.dma_start(lists["n2"][:], n2)
+        nc.sync.dma_start(lists["n3"][:], n3)
+        nc.sync.dma_start(out=gains_m[:], in_=gm.rearrange("(p t) o -> p (t o)", t=PACK))
+        load_scale_rows([nc.sync] * 4, raw_planes[:, 2, :], w3_scales)
+        load_scale_rows([nc.sync] * 4, raw_planes[:, 1, :], w2_scales)
+        nc.sync.dma_start(out=gains_n[:], in_=gn.rearrange("(p t) o -> p (t o)", t=PACK))
+        nc.sync.dma_start(lists["n1"][:], n1)
+        nc.sync.dma_start(lists["n6"][:], n6)
+        nc.sync.dma_start(lists["n5"][:], n5)
 
         four = sb("four", [P, 1], F32)
         half = sb("half", [P, 1], F32)
         nc.vector.memset(four[:], 4.0)
         nc.scalar.activation(out=half[:], in_=four[:], func=ACT.Abs_reciprocal_sqrt)
-
-        raw_words = [sb("raw_words%d" % w, [P, 2 * H], U8) for w in range(3)]
-        x_table = sb("x_table", [P, T], U32)
-        nc.sync.dma_start(lists["offs"][:], offs)
-        nc.sync.dma_start(out=raw_words[0][:].bitcast(I32), in_=w1_words[0].bitcast(I32))
-        load_scale_rows(nc.sync, x_plane, x_scales)
-        load_scale_rows(nc.gpsimd, raw_planes[:, 0, :], w1_scales)
-        nc.sync.dma_start(out=x_table[:].bitcast(I32), in_=x_words[0].rearrange("p n t -> p (n t)").bitcast(I32))
-        nc.sync.dma_start(lists["n4"][:], n4)
-        nc.sync.dma_start(lists["n2"][:], n2)
-        nc.sync.dma_start(lists["n3"][:], n3)
-        gains_m = sb("gains_m", [P, PACK], F32)
-        gains_n = sb("gains_n", [P, PACK], F32)
-        nc.sync.dma_start(out=raw_words[2][:].bitcast(I32), in_=w3_words[0].bitcast(I32))
-        load_scale_rows(nc.sync, raw_planes[:, 2, :], w3_scales)
-        nc.sync.dma_start(out=raw_words[1][:].bitcast(I32), in_=w2_words[0].bitcast(I32))
-        load_scale_rows(nc.sync, raw_planes[:, 1, :], w2_scales)
-        nc.sync.dma_start(out=gains_m[:], in_=gm.rearrange("(p t) o -> p (t o)", t=PACK))
-        nc.sync.dma_start(out=gains_n[:], in_=gn.rearrange("(p t) o -> p (t o)", t=PACK))
-        nc.sync.dma_start(lists["n1"][:], n1)
-        nc.sync.dma_start(lists["n6"][:], n6)
-        nc.sync.dma_start(lists["n5"][:], n5)
 
         y_win = [sb("y_win%d" % t, [P, 2 * S], F32) for t in range(PACK)]
         y_last = sb("y_last", [P, S], F32)
@@ -113,28 +116,29 @@ def tile_picked_forkmaxbfracwind_none_po_kernel(
 
         w_words = [sb("w_words%d" % w, [P, 2 * H], U8) for w in range(3)]
         w_plane = [sb("w_plane%d" % w, [P, H], U8) for w in range(3)]
-        deal(nc, w_words[0][:], w_plane[0][:], raw_words[0][:], raw_planes[:, 0, :])
+        deal_words(nc, w_words[0][:], raw_words[0][:])
 
         xq_scales = sb("xq_scales", [P, S], U8)
         xq_codes = sb("xq_codes", [P, S], U32)
         nc.vector.tensor_copy(xq_scales[:], x_plane[:].indirect(lists["offs"][:]))
         nc.vector.tensor_copy(xq_codes[:], x_table[:].indirect(lists["offs"][:]))
+        w1_dealt = raw_planes[:, 0, :].rearrange("p (m t) -> p t m", t=PACK)
+        nc.vector.tensor_copy(out=w_plane[0][:, :P], in_=w1_dealt[:, 0, :])
+        nc.vector.tensor_copy(out=w_plane[0][:, P:].rearrange("p (t m) -> p t m", m=P), in_=w1_dealt[:, 1:, :])
 
         y_bank = [psum.tile([P, S], F32, name="y_bank%d" % t, tag="low%d" % t) for t in range(PACK)]
         for t in range(PACK):
             product(nc, y_bank[t][:], w_words[0], w_plane[0], t, xq_codes[:], xq_scales[:])
-        deal(nc, w_words[2][:], w_plane[2][:], raw_words[2][:], raw_planes[:, 2, :])
-        deal(nc, w_words[1][:], w_plane[1][:], raw_words[1][:], raw_planes[:, 1, :])
+        deal_words(nc, w_words[2][:], raw_words[2][:])
+        deal_words(nc, w_words[1][:], raw_words[1][:])
 
         y4 = [sb("y4_%d" % t, [P, S], F32) for t in range(PACK)]
         d34 = [sb("d34_%d" % t, [P, S], F32) for t in range(PACK)]
         d2 = [sb("d2_%d" % t, [P, S], F32) for t in range(PACK)]
-        d1 = [sb("d1_%d" % t, [P, S], F32) for t in range(PACK)]
         dist = [sb("dist_%d" % t, [P, S], F32) for t in range(PACK)]
         den2 = [sb("den2_%d" % t, [P, S], F32) for t in range(PACK)]
         inv = [sb("inv_%d" % t, [P, S], F32) for t in range(PACK)]
         z2 = sb("z2", [P, PACK, S], F32)
-        z = sb("z", [P, PACK, S], F32)
 
         def z2_plane(t):
             nc.vector.scalar_tensor_tensor(
@@ -143,7 +147,7 @@ def tile_picked_forkmaxbfracwind_none_po_kernel(
 
         def z_plane(t):
             nc.vector.scalar_tensor_tensor(
-                out=z[:, t, :], in0=d1[t][:], scalar=gains_n[:, t : t + 1], in1=inv[t][:], op0=ALU.mult, op1=ALU.mult
+                out=z[:, t, :], in0=d1[:, t, :], scalar=gains_n[:, t : t + 1], in1=inv[t][:], op0=ALU.mult, op1=ALU.mult
             )
 
         for t in range(PACK):
@@ -159,16 +163,20 @@ def tile_picked_forkmaxbfracwind_none_po_kernel(
             nc.scalar.activation(out=den2[t][:], in_=dist[t][:], func=ACT.Square, bias=half[:])
             nc.scalar.activation(out=inv[t][:], in_=den2[t][:], func=ACT.Abs_reciprocal_sqrt)
 
+        deal_plane(nc, w_plane[2][:], raw_planes[:, 2, :])
+        deal_plane(nc, w_plane[1][:], raw_planes[:, 1, :])
+        d1 = sb("d1", [P, PACK, S], F32, tag="y4_3")
+
         def first_gather(t):
-            nc.vector.tensor_tensor(d1[t][:], y_win[t][:].indirect(lists["n1"][:]), y_plain[t], ALU.subtract)
+            nc.vector.tensor_tensor(d1[:, t, :], y_win[t][:].indirect(lists["n1"][:]), y_plain[t], ALU.subtract)
 
         first_gather(0)
         z2_plane(PACK - 1)
         z2_bf = sb("z2_bf", [P, PACK * S], BF16)
         interleave(nc, z2_bf[:], z2[:], 1.0)
         first_gather(1)
-        z_plane(0)
         first_gather(2)
+        first_gather(3)
         z2_codes = sb("z2_codes", [P, S], U32)
         z2_scales = sb("z2_scales", [P, S], U8)
         nc.vector.quantize_mx(out=z2_codes[:].bitcast(FP8X4), scales=z2_scales[:], in_=z2_bf[:])
@@ -177,14 +185,13 @@ def tile_picked_forkmaxbfracwind_none_po_kernel(
         for t in range(PACK):
             product(nc, b_bank[t][:], w_words[2], w_plane[2], t, z2_codes[:], z2_scales[:])
             nc.scalar.copy(out=b_win[t][:], in_=b_bank[t][:])
-        z_plane(1)
-        first_gather(3)
-        z_plane(2)
-        z_plane(3)
+        z = sb("z", [P, PACK, S], F32, tag="z2_bf")
+        for t in range(PACK):
+            z_plane(t)
         z_bf = sb("z_bf", [P, PACK * S], BF16)
         interleave(nc, z_bf[:], z[:], -1.0)
 
-        b6 = [sb("b6_%d" % t, [P, S], F32) for t in range(PACK)]
+        b6 = [sb("b6_%d" % t, [P, S], F32) for t in range(PACK - 1)]
 
         def cols(h):
             return slice(h * HALF, (h + 1) * HALF)
@@ -198,6 +205,7 @@ def tile_picked_forkmaxbfracwind_none_po_kernel(
 
         b_gather(0)
         b_gather(1)
+        b_gather(2)
         z_codes = sb("z_codes", [P, S], U32)
         z_scales = sb("z_scales", [P, S], U8)
         nc.vector.quantize_mx(out=z_codes[:].bitcast(FP8X4), scales=z_scales[:], in_=z_bf[:])
@@ -206,7 +214,7 @@ def tile_picked_forkmaxbfracwind_none_po_kernel(
         for t in range(PACK):
             product(nc, a_bank[t][:], w_words[1], w_plane[1], t, z_codes[:], z_scales[:])
             nc.scalar.copy(out=a_win[t][:], in_=a_bank[t][:])
-        b_gather(2)
+        b6.append(sb("b6_3", [P, S], F32, tag="z_bf"))
         b_gather(3)
 
         larger = [sb("larger%d" % t, [P, S], F32) for t in range(PACK)]
@@ -228,10 +236,17 @@ def tile_picked_forkmaxbfracwind_none_po_kernel(
                     nc.vector.tensor_tensor(smaller[t][:], a5[t][:], b_bank[t][:, cols(h)], ALU.min)
                 if step >= 2:
                     t = step - 2
-                    nc.vector.tensor_tensor(result[:, t, :], larger[t][:, cols(h)], smaller[t][:], ALU.subtract)
+                    engine = nc.gpsimd if h == 0 or t < 2 else nc.vector
+                    engine.tensor_tensor(result[:, t, :], larger[t][:, cols(h)], smaller[t][:], ALU.subtract)
                     nc.sync.dma_start(out=out_rows[:, t, cols(h)], in_=result[:, t, :])
             result_bf = sb("result_bf%d" % h, [P, PACK * HALF], BF16)
-            interleave(nc, result_bf[:], result[:], 1.0)
+            if h == 0:
+                interleave(nc, result_bf[:], result[:], 1.0)
+            else:
+                nc.vector.tensor_copy(
+                    out=result_bf[:].rearrange("p (c i t) -> p c t i", i=4, t=PACK),
+                    in_=result[:].rearrange("p t (c i) -> p c t i", i=4),
+                )
             nc.vector.quantize_mx(out=out_codes[:, cols(h)].bitcast(FP8X4), scales=out_scales[:, cols(h)], in_=result_bf[:])
             nc.sync.dma_start(out=out_words[:, cols(h)], in_=out_codes[:, cols(h)].bitcast(I32))
         for q in range(4):

@@ -26,15 +26,15 @@ def load_scale_rows(queues, plane, scales):
         queues[q].dma_start(out=plane[32 * q : 32 * q + 4, :].bitcast(I32), in_=scales[0, 4 * q : 4 * q + 4, :].bitcast(I32))
 
 
-def deal_words(nc, words, raw_words):
-    nc.vector.tensor_copy(
+def deal_words(engine, words, raw_words):
+    engine.tensor_copy(
         out=words.rearrange("p (t m b) -> p t m b", t=PACK, b=2),
         in_=raw_words.rearrange("p (m t b) -> p t m b", t=PACK, b=2),
     )
 
 
-def deal_plane(nc, plane, raw_plane):
-    nc.vector.tensor_copy(
+def deal_plane(engine, plane, raw_plane):
+    engine.tensor_copy(
         out=plane.rearrange("p (t m) -> p t m", t=PACK),
         in_=raw_plane.rearrange("p (m t) -> p t m", t=PACK),
     )
@@ -73,6 +73,12 @@ def tile_picked_forkmaxbfracwind_none_po_kernel(
         def sb(name, shape, dtype, tag=None):
             return keep.tile(shape, dtype, name=name, align_bytes=64, tag=tag or name)
 
+        def cols(h):
+            return slice(h * HALF, (h + 1) * HALF)
+
+        def entries(name, h):
+            return lists[name][:, h * HALF // 16 : (h + 1) * HALF // 16]
+
         lists = {}
         for name in ("offs", "n1", "n2", "n3", "n4", "n5", "n6"):
             lists[name] = keep.tile([P, S // 16], U16, name="list_" + name)
@@ -89,20 +95,20 @@ def tile_picked_forkmaxbfracwind_none_po_kernel(
         nc.sync.dma_start(lists["offs"][:], offs)
         nc.sync.dma_start(out=raw_words[0][:].bitcast(I32), in_=w1_words[0].bitcast(I32))
         load_scale_rows([nc.sync] * 4, x_plane, x_scales)
+        nc.sync.dma_start(out=raw_words[1][:].bitcast(I32), in_=w2_words[0].bitcast(I32))
         nc.sync.dma_start(out=x_table[:].bitcast(I32), in_=x_words[0].rearrange("p n t -> p (n t)").bitcast(I32))
         load_scale_rows([nc.sync] * 4, raw_planes[:, 0, :], w1_scales)
-        nc.sync.dma_start(out=raw_words[2][:].bitcast(I32), in_=w3_words[0].bitcast(I32))
-        nc.sync.dma_start(out=raw_words[1][:].bitcast(I32), in_=w2_words[0].bitcast(I32))
-        nc.sync.dma_start(lists["n4"][:], n4)
         nc.sync.dma_start(lists["n2"][:], n2)
-        nc.sync.dma_start(lists["n3"][:], n3)
-        nc.sync.dma_start(out=gains_m[:], in_=gm.rearrange("(p t) o -> p (t o)", t=PACK))
-        load_scale_rows([nc.sync] * 4, raw_planes[:, 2, :], w3_scales)
+        nc.sync.dma_start(lists["n1"][:], n1)
         load_scale_rows([nc.sync] * 4, raw_planes[:, 1, :], w2_scales)
         nc.sync.dma_start(out=gains_n[:], in_=gn.rearrange("(p t) o -> p (t o)", t=PACK))
-        nc.sync.dma_start(lists["n1"][:], n1)
-        nc.sync.dma_start(lists["n6"][:], n6)
+        nc.sync.dma_start(lists["n4"][:], n4)
+        nc.sync.dma_start(lists["n3"][:], n3)
+        nc.sync.dma_start(out=gains_m[:], in_=gm.rearrange("(p t) o -> p (t o)", t=PACK))
+        nc.sync.dma_start(out=raw_words[2][:].bitcast(I32), in_=w3_words[0].bitcast(I32))
+        load_scale_rows([nc.sync] * 4, raw_planes[:, 2, :], w3_scales)
         nc.sync.dma_start(lists["n5"][:], n5)
+        nc.sync.dma_start(lists["n6"][:], n6)
 
         four = sb("four", [P, 1], F32)
         half = sb("half", [P, 1], F32)
@@ -114,130 +120,132 @@ def tile_picked_forkmaxbfracwind_none_po_kernel(
         nc.gpsimd.memset(y_win[0][:, S:], 0.0)
         y_plain = [y_win[t + 1][:, S:] for t in range(PACK - 1)] + [y_last[:]]
 
-        w_words = [sb("w_words%d" % w, [P, 2 * H], U8) for w in range(3)]
-        w_plane = [sb("w_plane%d" % w, [P, H], U8) for w in range(3)]
-        deal_words(nc, w_words[0][:], raw_words[0][:])
+        w_words = [sb("w_words%d" % w, [P, 2 * H], U8) for w in range(2)]
+        w_plane = [sb("w_plane%d" % w, [P, H], U8) for w in range(2)]
+        deal_words(nc.vector, w_words[0][:], raw_words[0][:])
 
         xq_scales = sb("xq_scales", [P, S], U8)
         xq_codes = sb("xq_codes", [P, S], U32)
         nc.vector.tensor_copy(xq_scales[:], x_plane[:].indirect(lists["offs"][:]))
-        nc.vector.tensor_copy(xq_codes[:], x_table[:].indirect(lists["offs"][:]))
+        deal_words(nc.vector, w_words[1][:], raw_words[1][:])
         w1_dealt = raw_planes[:, 0, :].rearrange("p (m t) -> p t m", t=PACK)
-        nc.vector.tensor_copy(out=w_plane[0][:, :P], in_=w1_dealt[:, 0, :])
+        y_first = [psum.tile([P, HALF], F32, name="y_first%d" % h, tag="high%d" % h) for h in range(2)]
+        for h in range(2):
+            nc.vector.tensor_copy(xq_codes[:, cols(h)], x_table[:].indirect(entries("offs", h)))
+            if h == 0:
+                nc.vector.tensor_copy(out=w_plane[0][:, :P], in_=w1_dealt[:, 0, :])
+            product(nc, y_first[h][:], w_words[0], w_plane[0], 0, xq_codes[:, cols(h)], xq_scales[:, cols(h)])
         nc.vector.tensor_copy(out=w_plane[0][:, P:].rearrange("p (t m) -> p t m", m=P), in_=w1_dealt[:, 1:, :])
-
-        y_bank = [psum.tile([P, S], F32, name="y_bank%d" % t, tag="low%d" % t) for t in range(PACK)]
-        for t in range(PACK):
+        y_bank = [None] + [psum.tile([P, S], F32, name="y_bank%d" % t, tag="low%d" % t) for t in range(1, PACK)]
+        for t in range(1, PACK):
             product(nc, y_bank[t][:], w_words[0], w_plane[0], t, xq_codes[:], xq_scales[:])
-        deal_words(nc, w_words[2][:], raw_words[2][:])
-        deal_words(nc, w_words[1][:], raw_words[1][:])
 
-        y4 = [sb("y4_%d" % t, [P, S], F32) for t in range(PACK)]
-        d34 = [sb("d34_%d" % t, [P, S], F32) for t in range(PACK)]
+        d34 = [sb("d34_%d" % t, [P, S], F32) for t in range(PACK - 1)]
         d2 = [sb("d2_%d" % t, [P, S], F32) for t in range(PACK)]
+        d1 = [sb("d1_%d" % t, [P, S], F32) for t in range(PACK)]
         dist = [sb("dist_%d" % t, [P, S], F32) for t in range(PACK)]
         den2 = [sb("den2_%d" % t, [P, S], F32) for t in range(PACK)]
         inv = [sb("inv_%d" % t, [P, S], F32) for t in range(PACK)]
+        factor = [sb("factor_%d" % t, [P, S], F32) for t in range(PACK)]
         z2 = sb("z2", [P, PACK, S], F32)
 
-        def z2_plane(t):
-            nc.vector.scalar_tensor_tensor(
-                out=z2[:, t, :], in0=d34[t][:], scalar=gains_m[:, t : t + 1], in1=y_plain[t], op0=ALU.mult, op1=ALU.mult
-            )
-
-        def z_plane(t):
-            nc.vector.scalar_tensor_tensor(
-                out=z[:, t, :], in0=d1[:, t, :], scalar=gains_n[:, t : t + 1], in1=inv[t][:], op0=ALU.mult, op1=ALU.mult
-            )
-
-        for t in range(PACK):
+        for h in range(2):
+            nc.scalar.copy(out=y_win[0][:, cols(h)], in_=y_first[h][:])
+            nc.vector.tensor_copy(out=y_plain[0][:, cols(h)], in_=y_win[0][:, cols(h)])
+        for t in range(1, PACK):
             nc.scalar.copy(out=y_win[t][:, :S], in_=y_bank[t][:])
             nc.scalar.copy(out=y_plain[t], in_=y_bank[t][:])
         for t in range(PACK):
-            nc.vector.tensor_copy(y4[t][:], y_win[t][:].indirect(lists["n4"][:]))
-            if t > 0:
-                z2_plane(t - 1)
             nc.vector.tensor_tensor(d2[t][:], y_win[t][:].indirect(lists["n2"][:]), y_plain[t], ALU.subtract)
-            nc.vector.tensor_tensor(d34[t][:], y_win[t][:].indirect(lists["n3"][:]), y4[t][:], ALU.subtract)
+            nc.vector.tensor_tensor(d1[t][:], y_win[t][:].indirect(lists["n1"][:]), y_plain[t], ALU.subtract)
             nc.scalar.activation(out=dist[t][:], in_=d2[t][:], func=ACT.Abs)
             nc.scalar.activation(out=den2[t][:], in_=dist[t][:], func=ACT.Square, bias=half[:])
             nc.scalar.activation(out=inv[t][:], in_=den2[t][:], func=ACT.Abs_reciprocal_sqrt)
+            nc.scalar.activation(out=factor[t][:], in_=inv[t][:], func=ACT.Copy, scale=gains_n[:, t : t + 1])
 
-        deal_plane(nc, w_plane[2][:], raw_planes[:, 2, :])
-        deal_plane(nc, w_plane[1][:], raw_planes[:, 1, :])
-        d1 = sb("d1", [P, PACK, S], F32, tag="y4_3")
+        deal_plane(nc.vector, w_plane[1][:], raw_planes[:, 1, :])
+        z_y4 = sb("z_y4", [P, 2 * PACK, S], F32, tag="y_last")
+        for t in range(PACK):
+            nc.vector.tensor_copy(z_y4[:, PACK + t, :], y_win[t][:].indirect(lists["n4"][:]))
+            nc.gpsimd.tensor_tensor(z_y4[:, t, :], d1[t][:], factor[t][:], ALU.mult)
+        z_bf = sb("z_bf", [P, PACK * S], BF16)
+        interleave(nc, z_bf[:], z_y4[:, :PACK, :], -1.0)
 
-        def first_gather(t):
-            nc.vector.tensor_tensor(d1[:, t, :], y_win[t][:].indirect(lists["n1"][:]), y_plain[t], ALU.subtract)
+        def difference(t):
+            nc.vector.tensor_tensor(d34[t][:], y_win[t][:].indirect(lists["n3"][:]), z_y4[:, PACK + t, :], ALU.subtract)
 
-        first_gather(0)
-        z2_plane(PACK - 1)
+        def z2_plane(t):
+            nc.vector.scalar_tensor_tensor(
+                out=z2[:, t, :], in0=d34[t][:], scalar=gains_m[:, t : t + 1], in1=y_bank[t][:] if t else y_plain[0], op0=ALU.mult, op1=ALU.mult
+            )
+
+        difference(0)
+        difference(1)
+        z2_plane(0)
+        difference(2)
+        z2_plane(1)
+        z_codes = sb("z_codes", [P, S], U32)
+        z_scales = sb("z_scales", [P, S], U8)
+        nc.vector.quantize_mx(out=z_codes[:].bitcast(FP8X4), scales=z_scales[:], in_=z_bf[:])
+        a_bank = [psum.tile([P, S], F32, name="a_bank%d" % t, tag="high%d" % t) for t in range(PACK)]
+        for t in range(PACK):
+            product(nc, a_bank[t][:], w_words[1], w_plane[1], t, z_codes[:], z_scales[:])
+        d34.append(sb("d34_3", [P, S], F32, tag="z_bf"))
+        difference(3)
+        for t in range(PACK):
+            nc.scalar.copy(out=y_win[t][:, :S], in_=a_bank[t][:])
+        z2_plane(2)
+        z2_plane(3)
+        w_words.append(sb("w_words2", [P, 2 * H], U8, tag="y_last"))
+        w_plane.append(sb("w_plane2", [P, H], U8, tag="z_bf"))
+        raw_w3 = raw_words[2][:].rearrange("p (m t b) -> p t m b", t=PACK, b=2)
+        raw_s3 = raw_planes[:, 2, :].rearrange("p (m t) -> p t m", t=PACK)
+        for t in range(PACK):
+            nc.gpsimd.tensor_copy(out=w_words[2][:, 2 * P * t : 2 * P * (t + 1)].rearrange("p (m b) -> p m b", b=2), in_=raw_w3[:, t, :, :])
+            nc.gpsimd.tensor_copy(out=w_plane[2][:, P * t : P * (t + 1)], in_=raw_s3[:, t, :])
         z2_bf = sb("z2_bf", [P, PACK * S], BF16)
         interleave(nc, z2_bf[:], z2[:], 1.0)
-        first_gather(1)
-        first_gather(2)
-        first_gather(3)
+
+        a5 = [sb("a5_%d" % t, [P, S], F32) for t in range(PACK - 1)]
+
+        def a_gather(t):
+            nc.vector.tensor_copy(a5[t][:], y_win[t][:].indirect(lists["n5"][:]))
+
+        a_gather(0)
+        a_gather(1)
+        a_gather(2)
         z2_codes = sb("z2_codes", [P, S], U32)
         z2_scales = sb("z2_scales", [P, S], U8)
         nc.vector.quantize_mx(out=z2_codes[:].bitcast(FP8X4), scales=z2_scales[:], in_=z2_bf[:])
-        b_bank = [psum.tile([P, S], F32, name="b_bank%d" % t, tag="high%d" % t) for t in range(PACK)]
+        b_bank = [psum.tile([P, S], F32, name="b_bank%d" % t, tag="low%d" % t) for t in range(PACK)]
         b_win = [sb("b_win%d" % t, [P, S], F32) for t in range(PACK)]
         for t in range(PACK):
             product(nc, b_bank[t][:], w_words[2], w_plane[2], t, z2_codes[:], z2_scales[:])
             nc.scalar.copy(out=b_win[t][:], in_=b_bank[t][:])
-        z = sb("z", [P, PACK, S], F32, tag="z2_bf")
-        for t in range(PACK):
-            z_plane(t)
-        z_bf = sb("z_bf", [P, PACK * S], BF16)
-        interleave(nc, z_bf[:], z[:], -1.0)
+        a5.append(sb("a5_3", [P, S], F32, tag="z2_bf"))
+        a_gather(3)
 
-        b6 = [sb("b6_%d" % t, [P, S], F32) for t in range(PACK - 1)]
-
-        def cols(h):
-            return slice(h * HALF, (h + 1) * HALF)
-
-        def entries(name, h):
-            return lists[name][:, h * HALF // 16 : (h + 1) * HALF // 16]
-
-        def b_gather(t):
-            for h in range(2):
-                nc.vector.tensor_copy(b6[t][:, cols(h)], b_win[t][:].indirect(entries("n6", h)))
-
-        b_gather(0)
-        b_gather(1)
-        b_gather(2)
-        z_codes = sb("z_codes", [P, S], U32)
-        z_scales = sb("z_scales", [P, S], U8)
-        nc.vector.quantize_mx(out=z_codes[:].bitcast(FP8X4), scales=z_scales[:], in_=z_bf[:])
-        a_bank = [psum.tile([P, S], F32, name="a_bank%d" % t, tag="low%d" % t) for t in range(PACK)]
-        a_win = [sb("a_win%d" % t, [P, S], F32) for t in range(PACK)]
-        for t in range(PACK):
-            product(nc, a_bank[t][:], w_words[1], w_plane[1], t, z_codes[:], z_scales[:])
-            nc.scalar.copy(out=a_win[t][:], in_=a_bank[t][:])
-        b6.append(sb("b6_3", [P, S], F32, tag="z_bf"))
-        b_gather(3)
-
-        larger = [sb("larger%d" % t, [P, S], F32) for t in range(PACK)]
+        smaller = [sb("smaller%d" % t, [P, S], F32) for t in range(PACK)]
         out_codes = sb("out_codes", [P, S], U32)
         out_scales = sb("out_scales", [P, S], U8)
         out_rows = out_0.rearrange("(p t) j -> p t j", t=PACK)
         out_words = out_1[0].rearrange("p n t -> p (n t)").bitcast(I32)
         for h in range(2):
-            a5 = [sb("a5_%d_%d" % (h, t), [P, HALF], F32) for t in range(PACK)]
-            smaller = [sb("smaller%d_%d" % (h, t), [P, HALF], F32) for t in range(PACK)]
+            b6 = [sb("b6_%d_%d" % (h, t), [P, HALF], F32) for t in range(PACK)]
+            larger = [sb("larger%d_%d" % (h, t), [P, HALF], F32) for t in range(PACK)]
             result = sb("result%d" % h, [P, PACK, HALF], F32)
             for step in range(PACK + 2):
                 if step < PACK:
-                    nc.vector.tensor_copy(a5[step][:], a_win[step][:].indirect(entries("n5", h)))
+                    nc.vector.tensor_copy(b6[step][:], b_win[step][:].indirect(entries("n6", h)))
                     if h == 0:
-                        nc.vector.tensor_tensor(larger[step][:], b6[step][:], a_bank[step][:], ALU.max)
+                        nc.vector.tensor_tensor(smaller[step][:], a5[step][:], b_bank[step][:], ALU.min)
                 if 1 <= step <= PACK:
                     t = step - 1
-                    nc.vector.tensor_tensor(smaller[t][:], a5[t][:], b_bank[t][:, cols(h)], ALU.min)
+                    nc.vector.tensor_tensor(larger[t][:], b6[t][:], a_bank[t][:, cols(h)], ALU.max)
                 if step >= 2:
                     t = step - 2
                     engine = nc.gpsimd if h == 0 or t < 2 else nc.vector
-                    engine.tensor_tensor(result[:, t, :], larger[t][:, cols(h)], smaller[t][:], ALU.subtract)
+                    engine.tensor_tensor(result[:, t, :], larger[t][:], smaller[t][:, cols(h)], ALU.subtract)
                     nc.sync.dma_start(out=out_rows[:, t, cols(h)], in_=result[:, t, :])
             result_bf = sb("result_bf%d" % h, [P, PACK * HALF], BF16)
             if h == 0:

@@ -1,6 +1,7 @@
 from contextlib import ExitStack
 
 import concourse.mybir as mybir
+from concourse.masks import make_identity
 
 K, T, S, N, H = 512, 2048, 512, 512, 512
 FLOPS = 2 * K * H * S + 2 * 2 * H * N * S
@@ -18,33 +19,44 @@ ACT = mybir.ActivationFunctionType
 
 P = 128
 PACK = 4
+QUADRANTS = 4
 HALF = S // 2
+LINE = 4
+W1, W2, W3 = 0, 1, 2
 
 
-def load_scale_rows(queues, plane, scales):
-    for q in range(4):
-        queues[q].dma_start(out=plane[32 * q : 32 * q + 4, :].bitcast(I32), in_=scales[0, 4 * q : 4 * q + 4, :].bitcast(I32))
+def cols(h):
+    return slice(h * HALF, (h + 1) * HALF)
 
 
-def deal_words(engine, words, raw_words):
-    engine.tensor_copy(
-        out=words.rearrange("p (t m b) -> p t m b", t=PACK, b=2),
-        in_=raw_words.rearrange("p (m t b) -> p t m b", t=PACK, b=2),
+def block(h, c):
+    return slice((2 * h + c) * P, (2 * h + c + 1) * P)
+
+
+def load_scale_rows(nc, scale_tile, scales):
+    for q in range(QUADRANTS):
+        nc.sync.dma_start(out=scale_tile[32 * q : 32 * q + 4, :].bitcast(I32), in_=scales[0, 4 * q : 4 * q + 4, :].bitcast(I32))
+
+
+def deal_words(nc, dealt, raw):
+    nc.vector.tensor_copy(
+        out=dealt.rearrange("p (t m b) -> p t m b", t=PACK, b=2),
+        in_=raw.rearrange("p (m t b) -> p t m b", t=PACK, b=2),
     )
 
 
-def deal_plane(engine, plane, raw_plane):
-    engine.tensor_copy(
-        out=plane.rearrange("p (t m) -> p t m", t=PACK),
-        in_=raw_plane.rearrange("p (m t) -> p t m", t=PACK),
+def deal_scales(nc, dealt, raw, first, last):
+    nc.vector.tensor_copy(
+        out=dealt.rearrange("p (t m) -> p t m", t=PACK)[:, first:last, :],
+        in_=raw.rearrange("p (m t) -> p t m", t=PACK)[:, first:last, :],
     )
 
 
-def product(nc, bank, words, plane, t, codes, scales):
+def product(nc, out, w_words, w_scales, t, codes, scales):
     nc.tensor.matmul_mx(
-        out=bank,
-        lhsT=words[:, 2 * P * t : 2 * P * (t + 1)].bitcast(FP4X4),
-        lhsT_scale=plane[:, P * t : P * (t + 1)],
+        out=out,
+        lhsT=w_words[:, 2 * P * t : 2 * P * (t + 1)].bitcast(FP4X4),
+        lhsT_scale=w_scales[:, P * t : P * (t + 1)],
         rhs=codes.bitcast(FP8X4),
         rhs_scale=scales,
         start=True,
@@ -52,12 +64,10 @@ def product(nc, bank, words, plane, t, codes, scales):
     )
 
 
-def interleave(nc, grouped, planes, scale):
-    nc.scalar.activation(
-        out=grouped.rearrange("p (c i t) -> p c t i", i=4, t=PACK),
-        in_=planes.rearrange("p t (c i) -> p c t i", i=4),
-        func=ACT.Copy,
-        scale=scale,
+def weave(copy, woven, tiles):
+    copy(
+        out=woven.rearrange("p (c i t) -> p c t i", i=LINE, t=PACK),
+        in_=tiles.rearrange("p t (c i) -> p c t i", i=LINE),
     )
 
 
@@ -70,193 +80,233 @@ def tile_picked_forkmaxbfracwind_none_po_kernel(
         keep = ctx.enter_context(tc.tile_pool(name="keep", bufs=1))
         psum = ctx.enter_context(tc.psum_pool(name="psum", bufs=1))
 
-        def sb(name, shape, dtype, tag=None):
-            return keep.tile(shape, dtype, name=name, align_bytes=64, tag=tag or name)
+        def sb(name, shape, dtype, after=None):
+            return keep.tile(shape, dtype, name=name, align_bytes=64, tag=after or name)
 
-        def cols(h):
-            return slice(h * HALF, (h + 1) * HALF)
+        def bank(name, number, shape):
+            return psum.tile(shape, F32, name=name, tag="bank%d" % number)
 
-        def entries(name, h):
-            return lists[name][:, h * HALF // 16 : (h + 1) * HALF // 16]
+        def turn(out, in_, start, stop):
+            nc.tensor.matmul(out, lhsT=in_, rhs=identity[:], start=start, stop=stop, is_transpose=True)
 
         lists = {}
         for name in ("offs", "n1", "n2", "n3", "n4", "n5", "n6"):
             lists[name] = keep.tile([P, S // 16], U16, name="list_" + name)
 
-        x_plane = sb("x_plane", [P, T], U8)
-        raw_planes = sb("raw_planes", [P, 3, H], U8)
-        nc.gpsimd.memset(x_plane[:].bitcast(I32), 0)
-        nc.vector.memset(raw_planes[:].rearrange("p w n -> p (w n)").bitcast(I32), 0)
+        def entries(name, h):
+            return lists[name][:, h * HALF // 16 : (h + 1) * HALF // 16]
+
+        x_scale_table = sb("x_scale_table", [P, T], U8)
+        raw_scales = sb("raw_scales", [P, 3, H], U8)
+        nc.gpsimd.memset(x_scale_table[:].bitcast(I32), 0)
+        nc.vector.memset(raw_scales[:].rearrange("p w n -> p (w n)").bitcast(I32), 0)
 
         raw_words = [sb("raw_words%d" % w, [P, 2 * H], U8) for w in range(3)]
-        x_table = sb("x_table", [P, T], U32)
+        x_word_table = sb("x_word_table", [P, T], U32)
         gains_m = sb("gains_m", [P, PACK], F32)
         gains_n = sb("gains_n", [P, PACK], F32)
         nc.sync.dma_start(lists["offs"][:], offs)
-        nc.sync.dma_start(out=raw_words[0][:].bitcast(I32), in_=w1_words[0].bitcast(I32))
-        load_scale_rows([nc.sync] * 4, x_plane, x_scales)
-        nc.sync.dma_start(out=raw_words[1][:].bitcast(I32), in_=w2_words[0].bitcast(I32))
-        nc.sync.dma_start(out=x_table[:].bitcast(I32), in_=x_words[0].rearrange("p n t -> p (n t)").bitcast(I32))
-        load_scale_rows([nc.sync] * 4, raw_planes[:, 0, :], w1_scales)
+        nc.sync.dma_start(out=raw_words[W1][:].bitcast(I32), in_=w1_words[0].bitcast(I32))
+        load_scale_rows(nc, x_scale_table, x_scales)
+        nc.sync.dma_start(out=raw_words[W3][:].bitcast(I32), in_=w3_words[0].bitcast(I32))
+        nc.sync.dma_start(out=x_word_table[:].bitcast(I32), in_=x_words[0].rearrange("p n t -> p (n t)").bitcast(I32))
+        load_scale_rows(nc, raw_scales[:, W1, :], w1_scales)
+        nc.sync.dma_start(out=raw_words[W2][:].bitcast(I32), in_=w2_words[0].bitcast(I32))
         nc.sync.dma_start(lists["n2"][:], n2)
-        nc.sync.dma_start(lists["n1"][:], n1)
-        load_scale_rows([nc.sync] * 4, raw_planes[:, 1, :], w2_scales)
-        nc.sync.dma_start(out=gains_n[:], in_=gn.rearrange("(p t) o -> p (t o)", t=PACK))
-        nc.sync.dma_start(lists["n4"][:], n4)
-        nc.sync.dma_start(lists["n3"][:], n3)
         nc.sync.dma_start(out=gains_m[:], in_=gm.rearrange("(p t) o -> p (t o)", t=PACK))
-        nc.sync.dma_start(out=raw_words[2][:].bitcast(I32), in_=w3_words[0].bitcast(I32))
-        load_scale_rows([nc.sync] * 4, raw_planes[:, 2, :], w3_scales)
-        nc.sync.dma_start(lists["n5"][:], n5)
+        nc.sync.dma_start(lists["n3"][:], n3)
+        nc.sync.dma_start(lists["n4"][:], n4)
+        load_scale_rows(nc, raw_scales[:, W3, :], w3_scales)
+        load_scale_rows(nc, raw_scales[:, W2, :], w2_scales)
+        nc.sync.dma_start(out=gains_n[:], in_=gn.rearrange("(p t) o -> p (t o)", t=PACK))
+        nc.sync.dma_start(lists["n1"][:], n1)
         nc.sync.dma_start(lists["n6"][:], n6)
+        nc.sync.dma_start(lists["n5"][:], n5)
 
         four = sb("four", [P, 1], F32)
-        half = sb("half", [P, 1], F32)
+        one_half = sb("one_half", [P, 1], F32)
         nc.vector.memset(four[:], 4.0)
-        nc.scalar.activation(out=half[:], in_=four[:], func=ACT.Abs_reciprocal_sqrt)
+        nc.scalar.activation(out=one_half[:], in_=four[:], func=ACT.Abs_reciprocal_sqrt)
 
-        y_win = [sb("y_win%d" % t, [P, 2 * S], F32) for t in range(PACK)]
-        y_last = sb("y_last", [P, S], F32)
-        nc.gpsimd.memset(y_win[0][:, S:], 0.0)
-        y_plain = [y_win[t + 1][:, S:] for t in range(PACK - 1)] + [y_last[:]]
+        identity = sb("identity", [P, P], F32)
+        make_identity(nc, identity[:])
 
-        w_words = [sb("w_words%d" % w, [P, 2 * H], U8) for w in range(2)]
-        w_plane = [sb("w_plane%d" % w, [P, H], U8) for w in range(2)]
-        deal_words(nc.vector, w_words[0][:], raw_words[0][:])
+        wide = [sb("wide%d" % t, [P, 2 * S], F32) for t in range(PACK)]
+        gained_last = sb("gained_last", [P, S], F32)
+        nc.gpsimd.memset(wide[0][:, S:], 0.0)
+        gained = [wide[t + 1][:, S:] for t in range(PACK - 1)] + [gained_last[:]]
+        minus_y = [sb("minus_y%d" % t, [P, S], F32) for t in range(PACK)]
 
-        xq_scales = sb("xq_scales", [P, S], U8)
-        xq_codes = sb("xq_codes", [P, S], U32)
-        nc.vector.tensor_copy(xq_scales[:], x_plane[:].indirect(lists["offs"][:]))
-        deal_words(nc.vector, w_words[1][:], raw_words[1][:])
-        w1_dealt = raw_planes[:, 0, :].rearrange("p (m t) -> p t m", t=PACK)
-        y_first = [psum.tile([P, HALF], F32, name="y_first%d" % h, tag="high%d" % h) for h in range(2)]
+        w_words = [sb("w_words%d" % w, [P, 2 * H], U8) for w in range(3)]
+        w_scales = [sb("w_scales%d" % w, [P, H], U8) for w in range(3)]
+        deal_words(nc, w_words[W1][:], raw_words[W1][:])
+        picked_scales = sb("picked_scales", [P, S], U8)
+        picked_words = sb("picked_words", [P, S], U32)
+        nc.vector.tensor_copy(picked_scales[:], x_scale_table[:].indirect(lists["offs"][:]))
+        deal_words(nc, w_words[W3][:], raw_words[W3][:])
+        y_first = [bank("y_first%d" % h, 4 + h, [P, HALF]) for h in range(2)]
         for h in range(2):
-            nc.vector.tensor_copy(xq_codes[:, cols(h)], x_table[:].indirect(entries("offs", h)))
+            nc.vector.tensor_copy(picked_words[:, cols(h)], x_word_table[:].indirect(entries("offs", h)))
             if h == 0:
-                nc.vector.tensor_copy(out=w_plane[0][:, :P], in_=w1_dealt[:, 0, :])
-            product(nc, y_first[h][:], w_words[0], w_plane[0], 0, xq_codes[:, cols(h)], xq_scales[:, cols(h)])
-        nc.vector.tensor_copy(out=w_plane[0][:, P:].rearrange("p (t m) -> p t m", m=P), in_=w1_dealt[:, 1:, :])
-        y_bank = [None] + [psum.tile([P, S], F32, name="y_bank%d" % t, tag="low%d" % t) for t in range(1, PACK)]
+                deal_scales(nc, w_scales[W1][:], raw_scales[:, W1, :], 0, 1)
+            product(nc, y_first[h][:], w_words[W1], w_scales[W1], 0, picked_words[:, cols(h)], picked_scales[:, cols(h)])
+        deal_scales(nc, w_scales[W1][:], raw_scales[:, W1, :], 1, PACK)
+        y_bank = {t: bank("y_bank%d" % t, t, [P, S]) for t in range(1, PACK)}
         for t in range(1, PACK):
-            product(nc, y_bank[t][:], w_words[0], w_plane[0], t, xq_codes[:], xq_scales[:])
-
-        d34 = [sb("d34_%d" % t, [P, S], F32) for t in range(PACK - 1)]
-        d2 = [sb("d2_%d" % t, [P, S], F32) for t in range(PACK)]
-        d1 = [sb("d1_%d" % t, [P, S], F32) for t in range(PACK)]
-        dist = [sb("dist_%d" % t, [P, S], F32) for t in range(PACK)]
-        den2 = [sb("den2_%d" % t, [P, S], F32) for t in range(PACK)]
-        inv = [sb("inv_%d" % t, [P, S], F32) for t in range(PACK)]
-        factor = [sb("factor_%d" % t, [P, S], F32) for t in range(PACK)]
-        z2 = sb("z2", [P, PACK, S], F32)
+            product(nc, y_bank[t][:], w_words[W1], w_scales[W1], t, picked_words[:], picked_scales[:])
+        deal_words(nc, w_words[W2][:], raw_words[W2][:])
 
         for h in range(2):
-            nc.scalar.copy(out=y_win[0][:, cols(h)], in_=y_first[h][:])
-            nc.vector.tensor_copy(out=y_plain[0][:, cols(h)], in_=y_win[0][:, cols(h)])
+            nc.scalar.copy(out=wide[0][:, cols(h)], in_=y_first[h][:])
+            nc.vector.tensor_scalar(out=minus_y[0][:, cols(h)], in0=wide[0][:, cols(h)], scalar1=-1.0, scalar2=None, op0=ALU.mult)
+        nc.scalar.activation(out=gained[0], in_=wide[0][:, :S], func=ACT.Copy, scale=gains_m[:, 0:1])
         for t in range(1, PACK):
-            nc.scalar.copy(out=y_win[t][:, :S], in_=y_bank[t][:])
-            nc.scalar.copy(out=y_plain[t], in_=y_bank[t][:])
-        for t in range(PACK):
-            nc.vector.tensor_tensor(d2[t][:], y_win[t][:].indirect(lists["n2"][:]), y_plain[t], ALU.subtract)
-            nc.vector.tensor_tensor(d1[t][:], y_win[t][:].indirect(lists["n1"][:]), y_plain[t], ALU.subtract)
-            nc.scalar.activation(out=dist[t][:], in_=d2[t][:], func=ACT.Abs)
-            nc.scalar.activation(out=den2[t][:], in_=dist[t][:], func=ACT.Square, bias=half[:])
-            nc.scalar.activation(out=inv[t][:], in_=den2[t][:], func=ACT.Abs_reciprocal_sqrt)
-            nc.scalar.activation(out=factor[t][:], in_=inv[t][:], func=ACT.Copy, scale=gains_n[:, t : t + 1])
+            nc.scalar.copy(out=wide[t][:, :S], in_=y_bank[t][:])
+            nc.scalar.activation(out=minus_y[t][:], in_=y_bank[t][:], func=ACT.Copy, scale=-1.0)
+            nc.scalar.activation(out=gained[t], in_=y_bank[t][:], func=ACT.Copy, scale=gains_m[:, t : t + 1])
 
-        deal_plane(nc.vector, w_plane[1][:], raw_planes[:, 1, :])
-        z_y4 = sb("z_y4", [P, 2 * PACK, S], F32, tag="y_last")
-        for t in range(PACK):
-            nc.vector.tensor_copy(z_y4[:, PACK + t, :], y_win[t][:].indirect(lists["n4"][:]))
-            nc.gpsimd.tensor_tensor(z_y4[:, t, :], d1[t][:], factor[t][:], ALU.mult)
-        z_bf = sb("z_bf", [P, PACK * S], BF16)
-        interleave(nc, z_bf[:], z_y4[:, :PACK, :], -1.0)
-
-        def difference(t):
-            nc.vector.tensor_tensor(d34[t][:], y_win[t][:].indirect(lists["n3"][:]), z_y4[:, PACK + t, :], ALU.subtract)
-
-        def z2_plane(t):
-            nc.vector.scalar_tensor_tensor(
-                out=z2[:, t, :], in0=d34[t][:], scalar=gains_m[:, t : t + 1], in1=y_bank[t][:] if t else y_plain[0], op0=ALU.mult, op1=ALU.mult
+        diff2 = [sb("diff2_%d" % t, [P, S], F32) for t in range(PACK)]
+        distance = [sb("distance%d" % t, [P, S], F32) for t in range(PACK)]
+        squared = [sb("squared%d" % t, [P, S], F32) for t in range(PACK)]
+        inverse = [sb("inverse%d" % t, [P, S], F32) for t in range(PACK)]
+        term3 = [sb("term3_%d" % t, [P, S], F32) for t in range(PACK)]
+        term4 = [sb("term4_%d" % t, [P, S], F32) for t in range(PACK)]
+        word_bank = [bank("word_bank%d" % h, 6 + h, [P, 2, 2, P]) for h in range(2)]
+        for u in range(2):
+            z2_turned = [bank("z2_turned%d_%d" % (u, h), 2 * u + h, [P, 2, 2, P]) for h in range(2)]
+            for e in range(2):
+                t = 2 * u + e
+                nc.vector.tensor_tensor(diff2[t][:], wide[t][:].indirect(lists["n2"][:]), minus_y[t][:], ALU.add)
+                nc.vector.tensor_tensor(term3[t][:], wide[t][:].indirect(lists["n3"][:]), gained[t], ALU.mult)
+                nc.scalar.activation(out=distance[t][:], in_=diff2[t][:], func=ACT.Abs)
+                nc.scalar.activation(out=squared[t][:], in_=distance[t][:], func=ACT.Square, bias=one_half[:])
+                nc.scalar.activation(out=inverse[t][:], in_=squared[t][:], func=ACT.Abs_reciprocal_sqrt)
+                for h in range(2):
+                    nc.vector.tensor_tensor(term4[t][:, cols(h)], minus_y[t][:].indirect(entries("n4", h)), gained[t][:, cols(h)], ALU.mult)
+                    for c in range(2):
+                        turn(z2_turned[h][:, c, e, :], term3[t][:, block(h, c)], True, False)
+                        turn(z2_turned[h][:, c, e, :], term4[t][:, block(h, c)], False, True)
+            for h in range(2):
+                pairs = sb("pairs%d_%d" % (u, h), [P, 2, P, 2], BF16)
+                nc.scalar.copy(out=pairs[:], in_=z2_turned[h][:].rearrange("j c e p -> j c p e"))
+                pair_words = pairs[:].rearrange("j c p e -> j (c p e)").bitcast(F32)
+                for c in range(2):
+                    nc.tensor.transpose(word_bank[h][:, u, c, :], pair_words[:, c * P : (c + 1) * P], identity[:])
+        z2_woven = sb("z2_woven", [P, PACK * S], BF16)
+        for h in range(2):
+            nc.scalar.copy(
+                out=z2_woven[:, h * PACK * HALF : (h + 1) * PACK * HALF].bitcast(F32).rearrange("p (j u) -> p j u", u=2),
+                in_=word_bank[h][:].rearrange("p u c j -> p (c j) u"),
             )
+        deal_scales(nc, w_scales[W3][:], raw_scales[:, W3, :], 0, PACK)
+        deal_scales(nc, w_scales[W2][:], raw_scales[:, W2, :], 0, PACK)
 
-        difference(0)
-        difference(1)
-        z2_plane(0)
-        difference(2)
-        z2_plane(1)
-        z_codes = sb("z_codes", [P, S], U32)
-        z_scales = sb("z_scales", [P, S], U8)
-        nc.vector.quantize_mx(out=z_codes[:].bitcast(FP8X4), scales=z_scales[:], in_=z_bf[:])
-        a_bank = [psum.tile([P, S], F32, name="a_bank%d" % t, tag="high%d" % t) for t in range(PACK)]
+        diff1 = sb("diff1", [P, PACK, S], F32, after="gained_last")
         for t in range(PACK):
-            product(nc, a_bank[t][:], w_words[1], w_plane[1], t, z_codes[:], z_scales[:])
-        d34.append(sb("d34_3", [P, S], F32, tag="z_bf"))
-        difference(3)
-        for t in range(PACK):
-            nc.scalar.copy(out=y_win[t][:, :S], in_=a_bank[t][:])
-        z2_plane(2)
-        z2_plane(3)
-        w_words.append(sb("w_words2", [P, 2 * H], U8, tag="y_last"))
-        w_plane.append(sb("w_plane2", [P, H], U8, tag="z_bf"))
-        raw_w3 = raw_words[2][:].rearrange("p (m t b) -> p t m b", t=PACK, b=2)
-        raw_s3 = raw_planes[:, 2, :].rearrange("p (m t) -> p t m", t=PACK)
-        for t in range(PACK):
-            nc.gpsimd.tensor_copy(out=w_words[2][:, 2 * P * t : 2 * P * (t + 1)].rearrange("p (m b) -> p m b", b=2), in_=raw_w3[:, t, :, :])
-            nc.gpsimd.tensor_copy(out=w_plane[2][:, P * t : P * (t + 1)], in_=raw_s3[:, t, :])
-        z2_bf = sb("z2_bf", [P, PACK * S], BF16)
-        interleave(nc, z2_bf[:], z2[:], 1.0)
+            nc.vector.tensor_tensor(diff1[:, t, :], wide[t][:].indirect(lists["n1"][:]), minus_y[t][:], ALU.add)
 
-        a5 = [sb("a5_%d" % t, [P, S], F32) for t in range(PACK - 1)]
-
-        def a_gather(t):
-            nc.vector.tensor_copy(a5[t][:], y_win[t][:].indirect(lists["n5"][:]))
-
-        a_gather(0)
-        a_gather(1)
-        a_gather(2)
+        b_banks = (4, 5, 0, 1)
+        a_banks = (2, 3, 6, 7)
         z2_codes = sb("z2_codes", [P, S], U32)
         z2_scales = sb("z2_scales", [P, S], U8)
-        nc.vector.quantize_mx(out=z2_codes[:].bitcast(FP8X4), scales=z2_scales[:], in_=z2_bf[:])
-        b_bank = [psum.tile([P, S], F32, name="b_bank%d" % t, tag="low%d" % t) for t in range(PACK)]
-        b_win = [sb("b_win%d" % t, [P, S], F32) for t in range(PACK)]
+        nc.vector.quantize_mx(out=z2_codes[:].bitcast(FP8X4), scales=z2_scales[:], in_=z2_woven[:])
         for t in range(PACK):
-            product(nc, b_bank[t][:], w_words[2], w_plane[2], t, z2_codes[:], z2_scales[:])
-            nc.scalar.copy(out=b_win[t][:], in_=b_bank[t][:])
-        a5.append(sb("a5_3", [P, S], F32, tag="z2_bf"))
-        a_gather(3)
+            b_bank = bank("b_bank%d" % t, b_banks[t], [P, S])
+            product(nc, b_bank[:], w_words[W3], w_scales[W3], t, z2_codes[:], z2_scales[:])
+            nc.scalar.copy(out=wide[t][:, :S], in_=b_bank[:])
 
-        smaller = [sb("smaller%d" % t, [P, S], F32) for t in range(PACK)]
+        minus_z = sb("minus_z", [P, PACK, S], F32, after="z2_woven")
+        for t in range(PACK):
+            nc.vector.scalar_tensor_tensor(
+                out=minus_z[:, t, :], in0=diff1[:, t, :], scalar=gains_n[:, t : t + 1], in1=inverse[t][:], op0=ALU.mult, op1=ALU.mult
+            )
+        z_woven = sb("z_woven", [P, PACK * S], BF16)
+        weave(nc.scalar.copy, z_woven[:], minus_z[:])
+
+        b6 = [sb("b6_%d" % t, [P, S], F32) for t in range(PACK - 1)]
+        for t in range(PACK - 1):
+            nc.vector.tensor_copy(b6[t][:], wide[t][:].indirect(lists["n6"][:]))
+        z_codes = sb("z_codes", [P, S], U32)
+        z_scales = sb("z_scales", [P, S], U8)
+        nc.vector.quantize_mx(out=z_codes[:].bitcast(FP8X4), scales=z_scales[:], in_=z_woven[:])
+        b6.append(sb("b6_last", [P, S], F32, after="z_woven"))
+        nc.vector.tensor_copy(b6[PACK - 1][:], wide[PACK - 1][:].indirect(lists["n6"][:]))
+
+        def blocks(h, u):
+            return [(e, c, 2 * u + e) for e in range(2) for c in range(2)]
+
+        quarters = [(h, u) for u in range(2) for h in range(2)]
+        gap_turned = {}
+        for number, (h, u) in enumerate(quarters):
+            gap_turned[h, u] = bank("gap_turned%d_%d" % (h, u), b_banks[number], [P, 2, 2, P])
+            for e, c, t in blocks(h, u):
+                turn(gap_turned[h, u][:, e, c, :], wide[t][:, block(h, c)], e == 0 and c == 0, False)
+
+        minus_a = [sb("minus_a%d" % t, [P, S], F32) for t in range(PACK)]
+        minus_larger = [sb("minus_larger%d" % t, [P, S], F32) for t in range(PACK)]
+        for t in range(PACK):
+            a_bank = bank("a_bank%d" % t, a_banks[t], [P, S])
+            product(nc, a_bank[:], w_words[W2], w_scales[W2], t, z_codes[:], z_scales[:])
+            nc.vector.scalar_tensor_tensor(
+                out=minus_larger[t][:], in0=b6[t][:], scalar=-1.0, in1=a_bank[:], op0=ALU.mult, op1=ALU.min
+            )
+            nc.scalar.copy(out=minus_a[t][:], in_=a_bank[:])
+
+        staged = {}
+        for h, u in quarters:
+            for e, c, t in blocks(h, u):
+                turn(gap_turned[h, u][:, e, c, :], minus_larger[t][:, block(h, c)], False, e == 1 and c == 1)
+            staged[h, u] = sb("staged%d_%d" % (h, u), [P, 2, 2, P], F32)
+            nc.scalar.copy(out=staged[h, u][:], in_=gap_turned[h, u][:])
+        gap = {}
+        for number, (h, u) in enumerate(sorted(quarters)):
+            gap[h, u] = bank("gap%d_%d" % (h, u), a_banks[number], [P, 2, 2, P])
+            for e, c, t in blocks(h, u):
+                nc.tensor.transpose(gap[h, u][:, e, c, :], staged[h, u][:, e, c, :], identity[:])
+
         out_codes = sb("out_codes", [P, S], U32)
         out_scales = sb("out_scales", [P, S], U8)
         out_rows = out_0.rearrange("(p t) j -> p t j", t=PACK)
         out_words = out_1[0].rearrange("p n t -> p (n t)").bitcast(I32)
-        for h in range(2):
-            b6 = [sb("b6_%d_%d" % (h, t), [P, HALF], F32) for t in range(PACK)]
-            larger = [sb("larger%d_%d" % (h, t), [P, HALF], F32) for t in range(PACK)]
-            result = sb("result%d" % h, [P, PACK, HALF], F32)
-            for step in range(PACK + 2):
-                if step < PACK:
-                    nc.vector.tensor_copy(b6[step][:], b_win[step][:].indirect(entries("n6", h)))
-                    if h == 0:
-                        nc.vector.tensor_tensor(smaller[step][:], a5[step][:], b_bank[step][:], ALU.min)
-                if 1 <= step <= PACK:
-                    t = step - 1
-                    nc.vector.tensor_tensor(larger[t][:], b6[t][:], a_bank[t][:, cols(h)], ALU.max)
-                if step >= 2:
-                    t = step - 2
-                    engine = nc.gpsimd if h == 0 or t < 2 else nc.vector
-                    engine.tensor_tensor(result[:, t, :], larger[t][:], smaller[t][:, cols(h)], ALU.subtract)
-                    nc.sync.dma_start(out=out_rows[:, t, cols(h)], in_=result[:, t, :])
-            result_bf = sb("result_bf%d" % h, [P, PACK * HALF], BF16)
-            if h == 0:
-                interleave(nc, result_bf[:], result[:], 1.0)
-            else:
-                nc.vector.tensor_copy(
-                    out=result_bf[:].rearrange("p (c i t) -> p c t i", i=4, t=PACK),
-                    in_=result[:].rearrange("p t (c i) -> p c t i", i=4),
-                )
-            nc.vector.quantize_mx(out=out_codes[:, cols(h)].bitcast(FP8X4), scales=out_scales[:, cols(h)], in_=result_bf[:])
+        excess = {}
+        result = [sb("result%d" % h, [P, PACK, HALF], F32) for h in range(2)]
+
+        def look_up(h, t, after=None):
+            excess[h, t] = sb("excess%d_%d" % (h, t), [P, HALF], F32, after=after)
+            nc.vector.tensor_tensor(excess[h, t][:], minus_a[t][:].indirect(entries("n5", h)), wide[t][:, cols(h)], ALU.add)
+
+        def join(h, t):
+            nc.vector.scalar_tensor_tensor(
+                out=result[h][:, t, :],
+                in0=excess[h, t][:],
+                scalar=0.0,
+                in1=gap[h, t // 2][:, t % 2, :, :].rearrange("p c j -> p (c j)"),
+                op0=ALU.max,
+                op1=ALU.subtract,
+            )
+            nc.sync.dma_start(out=out_rows[:, t, cols(h)], in_=result[h][:, t, :])
+
+        def hand_on(h, copy):
+            result_woven = sb("result_woven%d" % h, [P, PACK * HALF], BF16)
+            weave(copy, result_woven[:], result[h][:])
+            nc.vector.quantize_mx(out=out_codes[:, cols(h)].bitcast(FP8X4), scales=out_scales[:, cols(h)], in_=result_woven[:])
             nc.sync.dma_start(out=out_words[:, cols(h)], in_=out_codes[:, cols(h)].bitcast(I32))
-        for q in range(4):
+
+        for t in range(PACK):
+            look_up(0, t)
+        look_up(1, 0)
+        look_up(1, 1)
+        join(0, 0)
+        join(0, 1)
+        look_up(1, 2, after="excess0_1")
+        join(0, 2)
+        join(0, 3)
+        look_up(1, 3, after="excess0_3")
+        hand_on(0, nc.scalar.copy)
+        for t in range(PACK):
+            join(1, t)
+        hand_on(1, nc.vector.tensor_copy)
+
+        for q in range(QUADRANTS):
             queue = nc.sync if q % 2 == 0 else nc.scalar
             queue.dma_start(out=out_2[0, 4 * q : 4 * q + 4, :].bitcast(I32), in_=out_scales[32 * q : 32 * q + 4, :].bitcast(I32))

from contextlib import ExitStack

import concourse.mybir as mybir
from concourse.masks import make_identity

K, T, S, N, H = 512, 2048, 512, 512, 512
FLOPS = 2 * K * H * S + 2 * 2 * H * N * S

F32 = mybir.dt.float32
BF16 = mybir.dt.bfloat16
I32 = mybir.dt.int32
U32 = mybir.dt.uint32
U16 = mybir.dt.uint16
U8 = mybir.dt.uint8
FP8X4 = mybir.dt.float8_e4m3fn_x4
FP4X4 = mybir.dt.float4_e2m1fn_x4
ALU = mybir.AluOpType
ACT = mybir.ActivationFunctionType

P = 128
PACK = 4
QUADRANTS = 4
HALF = S // 2
LINE = 4
W1, W2, W3 = 0, 1, 2


def cols(h):
    return slice(h * HALF, (h + 1) * HALF)


def block(h, c):
    return slice((2 * h + c) * P, (2 * h + c + 1) * P)


def load_scale_rows(nc, scale_tile, scales):
    for q in range(QUADRANTS):
        nc.sync.dma_start(out=scale_tile[32 * q : 32 * q + 4, :].bitcast(I32), in_=scales[0, 4 * q : 4 * q + 4, :].bitcast(I32))


def deal_words(nc, dealt, raw):
    nc.vector.tensor_copy(
        out=dealt.rearrange("p (t m b) -> p t m b", t=PACK, b=2),
        in_=raw.rearrange("p (m t b) -> p t m b", t=PACK, b=2),
    )


def deal_scales(nc, dealt, raw, first, last):
    nc.vector.tensor_copy(
        out=dealt.rearrange("p (t m) -> p t m", t=PACK)[:, first:last, :],
        in_=raw.rearrange("p (m t) -> p t m", t=PACK)[:, first:last, :],
    )


def product(nc, out, w_words, w_scales, t, codes, scales):
    nc.tensor.matmul_mx(
        out=out,
        lhsT=w_words[:, 2 * P * t : 2 * P * (t + 1)].bitcast(FP4X4),
        lhsT_scale=w_scales[:, P * t : P * (t + 1)],
        rhs=codes.bitcast(FP8X4),
        rhs_scale=scales,
        start=True,
        stop=True,
    )


def weave(copy, woven, tiles):
    copy(
        out=woven.rearrange("p (c i t) -> p c t i", i=LINE, t=PACK),
        in_=tiles.rearrange("p t (c i) -> p c t i", i=LINE),
    )


def tile_picked_forkmaxbfracwind_none_po_kernel(
    tc, x_words, x_scales, w1_words, w1_scales, gn, w2_words, w2_scales, gm, w3_words, w3_scales,
    offs, n1, n2, n3, n4, n5, n6, out_0, out_1, out_2,
):
    nc = tc.nc
    with ExitStack() as ctx:
        keep = ctx.enter_context(tc.tile_pool(name="keep", bufs=1))
        psum = ctx.enter_context(tc.psum_pool(name="psum", bufs=1))

        def sb(name, shape, dtype, after=None):
            return keep.tile(shape, dtype, name=name, align_bytes=64, tag=after or name)

        def bank(name, number, shape):
            return psum.tile(shape, F32, name=name, tag="bank%d" % number)

        def turn(out, in_, start, stop):
            nc.tensor.matmul(out, lhsT=in_, rhs=identity[:], start=start, stop=stop, is_transpose=True)

        lists = {}
        for name in ("offs", "n1", "n2", "n3", "n4", "n5", "n6"):
            lists[name] = keep.tile([P, S // 16], U16, name="list_" + name)

        def entries(name, h):
            return lists[name][:, h * HALF // 16 : (h + 1) * HALF // 16]

        x_scale_table = sb("x_scale_table", [P, T], U8)
        raw_scales = sb("raw_scales", [P, 3, H], U8)
        nc.gpsimd.memset(x_scale_table[:].bitcast(I32), 0)
        nc.vector.memset(raw_scales[:].rearrange("p w n -> p (w n)").bitcast(I32), 0)

        raw_words = [sb("raw_words%d" % w, [P, 2 * H], U8) for w in range(3)]
        x_word_table = sb("x_word_table", [P, T], U32)
        gains_m = sb("gains_m", [P, PACK], F32)
        gains_n = sb("gains_n", [P, PACK], F32)
        nc.sync.dma_start(lists["offs"][:], offs)
        nc.sync.dma_start(out=raw_words[W1][:].bitcast(I32), in_=w1_words[0].bitcast(I32))
        load_scale_rows(nc, x_scale_table, x_scales)
        nc.sync.dma_start(out=raw_words[W3][:].bitcast(I32), in_=w3_words[0].bitcast(I32))
        nc.sync.dma_start(out=x_word_table[:].bitcast(I32), in_=x_words[0].rearrange("p n t -> p (n t)").bitcast(I32))
        load_scale_rows(nc, raw_scales[:, W1, :], w1_scales)
        nc.sync.dma_start(out=raw_words[W2][:].bitcast(I32), in_=w2_words[0].bitcast(I32))
        nc.sync.dma_start(lists["n2"][:], n2)
        nc.sync.dma_start(out=gains_m[:], in_=gm.rearrange("(p t) o -> p (t o)", t=PACK))
        nc.sync.dma_start(lists["n3"][:], n3)
        nc.sync.dma_start(lists["n4"][:], n4)
        load_scale_rows(nc, raw_scales[:, W3, :], w3_scales)
        load_scale_rows(nc, raw_scales[:, W2, :], w2_scales)
        nc.sync.dma_start(out=gains_n[:], in_=gn.rearrange("(p t) o -> p (t o)", t=PACK))
        nc.sync.dma_start(lists["n1"][:], n1)
        nc.sync.dma_start(lists["n6"][:], n6)
        nc.sync.dma_start(lists["n5"][:], n5)

        four = sb("four", [P, 1], F32)
        one_half = sb("one_half", [P, 1], F32)
        nc.vector.memset(four[:], 4.0)
        nc.scalar.activation(out=one_half[:], in_=four[:], func=ACT.Abs_reciprocal_sqrt)

        identity = sb("identity", [P, P], F32)
        make_identity(nc, identity[:])

        wide = [sb("wide%d" % t, [P, 2 * S], F32) for t in range(PACK)]
        gained_last = sb("gained_last", [P, S], F32)
        nc.gpsimd.memset(wide[0][:, S:], 0.0)
        gained = [wide[t + 1][:, S:] for t in range(PACK - 1)] + [gained_last[:]]
        minus_y = [sb("minus_y%d" % t, [P, S], F32) for t in range(PACK)]

        w_words = [sb("w_words%d" % w, [P, 2 * H], U8) for w in range(3)]
        w_scales = [sb("w_scales%d" % w, [P, H], U8) for w in range(3)]
        deal_words(nc, w_words[W1][:], raw_words[W1][:])
        picked_scales = sb("picked_scales", [P, S], U8)
        picked_words = sb("picked_words", [P, S], U32)
        nc.vector.tensor_copy(picked_scales[:], x_scale_table[:].indirect(lists["offs"][:]))
        deal_words(nc, w_words[W3][:], raw_words[W3][:])
        y_first = [bank("y_first%d" % h, 4 + h, [P, HALF]) for h in range(2)]
        for h in range(2):
            nc.vector.tensor_copy(picked_words[:, cols(h)], x_word_table[:].indirect(entries("offs", h)))
            if h == 0:
                deal_scales(nc, w_scales[W1][:], raw_scales[:, W1, :], 0, 1)
            product(nc, y_first[h][:], w_words[W1], w_scales[W1], 0, picked_words[:, cols(h)], picked_scales[:, cols(h)])
        deal_scales(nc, w_scales[W1][:], raw_scales[:, W1, :], 1, PACK)
        y_bank = {t: bank("y_bank%d" % t, t, [P, S]) for t in range(1, PACK)}
        for t in range(1, PACK):
            product(nc, y_bank[t][:], w_words[W1], w_scales[W1], t, picked_words[:], picked_scales[:])
        deal_words(nc, w_words[W2][:], raw_words[W2][:])

        for h in range(2):
            nc.scalar.copy(out=wide[0][:, cols(h)], in_=y_first[h][:])
            nc.vector.tensor_scalar(out=minus_y[0][:, cols(h)], in0=wide[0][:, cols(h)], scalar1=-1.0, scalar2=None, op0=ALU.mult)
        nc.scalar.activation(out=gained[0], in_=wide[0][:, :S], func=ACT.Copy, scale=gains_m[:, 0:1])
        for t in range(1, PACK):
            nc.scalar.copy(out=wide[t][:, :S], in_=y_bank[t][:])
            nc.scalar.activation(out=minus_y[t][:], in_=y_bank[t][:], func=ACT.Copy, scale=-1.0)
            nc.scalar.activation(out=gained[t], in_=y_bank[t][:], func=ACT.Copy, scale=gains_m[:, t : t + 1])

        diff2 = [sb("diff2_%d" % t, [P, S], F32) for t in range(PACK)]
        distance = [sb("distance%d" % t, [P, S], F32) for t in range(PACK)]
        squared = [sb("squared%d" % t, [P, S], F32) for t in range(PACK)]
        inverse = [sb("inverse%d" % t, [P, S], F32) for t in range(PACK)]
        term3 = [sb("term3_%d" % t, [P, S], F32) for t in range(PACK)]
        term4 = [sb("term4_%d" % t, [P, S], F32) for t in range(PACK)]
        word_bank = [bank("word_bank%d" % h, 6 + h, [P, 2, 2, P]) for h in range(2)]
        for u in range(2):
            z2_turned = [bank("z2_turned%d_%d" % (u, h), 2 * u + h, [P, 2, 2, P]) for h in range(2)]
            for e in range(2):
                t = 2 * u + e
                nc.vector.tensor_tensor(diff2[t][:], wide[t][:].indirect(lists["n2"][:]), minus_y[t][:], ALU.add)
                nc.vector.tensor_tensor(term3[t][:], wide[t][:].indirect(lists["n3"][:]), gained[t], ALU.mult)
                nc.scalar.activation(out=distance[t][:], in_=diff2[t][:], func=ACT.Abs)
                nc.scalar.activation(out=squared[t][:], in_=distance[t][:], func=ACT.Square, bias=one_half[:])
                nc.scalar.activation(out=inverse[t][:], in_=squared[t][:], func=ACT.Abs_reciprocal_sqrt)
                for h in range(2):
                    nc.vector.tensor_tensor(term4[t][:, cols(h)], minus_y[t][:].indirect(entries("n4", h)), gained[t][:, cols(h)], ALU.mult)
                    for c in range(2):
                        turn(z2_turned[h][:, c, e, :], term3[t][:, block(h, c)], True, False)
                        turn(z2_turned[h][:, c, e, :], term4[t][:, block(h, c)], False, True)
            for h in range(2):
                pairs = sb("pairs%d_%d" % (u, h), [P, 2, P, 2], BF16)
                nc.scalar.copy(out=pairs[:], in_=z2_turned[h][:].rearrange("j c e p -> j c p e"))
                pair_words = pairs[:].rearrange("j c p e -> j (c p e)").bitcast(F32)
                for c in range(2):
                    nc.tensor.transpose(word_bank[h][:, u, c, :], pair_words[:, c * P : (c + 1) * P], identity[:])
        z2_woven = sb("z2_woven", [P, PACK * S], BF16)
        for h in range(2):
            nc.scalar.copy(
                out=z2_woven[:, h * PACK * HALF : (h + 1) * PACK * HALF].bitcast(F32).rearrange("p (j u) -> p j u", u=2),
                in_=word_bank[h][:].rearrange("p u c j -> p (c j) u"),
            )
        deal_scales(nc, w_scales[W3][:], raw_scales[:, W3, :], 0, PACK)
        deal_scales(nc, w_scales[W2][:], raw_scales[:, W2, :], 0, PACK)

        diff1 = sb("diff1", [P, PACK, S], F32, after="gained_last")
        for t in range(PACK):
            nc.vector.tensor_tensor(diff1[:, t, :], wide[t][:].indirect(lists["n1"][:]), minus_y[t][:], ALU.add)

        b_banks = (4, 5, 0, 1)
        a_banks = (2, 3, 6, 7)
        z2_codes = sb("z2_codes", [P, S], U32)
        z2_scales = sb("z2_scales", [P, S], U8)
        nc.vector.quantize_mx(out=z2_codes[:].bitcast(FP8X4), scales=z2_scales[:], in_=z2_woven[:])
        for t in range(PACK):
            b_bank = bank("b_bank%d" % t, b_banks[t], [P, S])
            product(nc, b_bank[:], w_words[W3], w_scales[W3], t, z2_codes[:], z2_scales[:])
            nc.scalar.copy(out=wide[t][:, :S], in_=b_bank[:])

        minus_z = sb("minus_z", [P, PACK, S], F32, after="z2_woven")
        for t in range(PACK):
            nc.vector.scalar_tensor_tensor(
                out=minus_z[:, t, :], in0=diff1[:, t, :], scalar=gains_n[:, t : t + 1], in1=inverse[t][:], op0=ALU.mult, op1=ALU.mult
            )
        z_woven = sb("z_woven", [P, PACK * S], BF16)
        weave(nc.scalar.copy, z_woven[:], minus_z[:])

        b6 = [sb("b6_%d" % t, [P, S], F32) for t in range(PACK - 1)]
        for t in range(PACK - 1):
            nc.vector.tensor_copy(b6[t][:], wide[t][:].indirect(lists["n6"][:]))
        z_codes = sb("z_codes", [P, S], U32)
        z_scales = sb("z_scales", [P, S], U8)
        nc.vector.quantize_mx(out=z_codes[:].bitcast(FP8X4), scales=z_scales[:], in_=z_woven[:])
        b6.append(sb("b6_last", [P, S], F32, after="z_woven"))
        nc.vector.tensor_copy(b6[PACK - 1][:], wide[PACK - 1][:].indirect(lists["n6"][:]))

        def blocks(h, u):
            return [(e, c, 2 * u + e) for e in range(2) for c in range(2)]

        quarters = [(h, u) for u in range(2) for h in range(2)]
        gap_turned = {}
        for number, (h, u) in enumerate(quarters):
            gap_turned[h, u] = bank("gap_turned%d_%d" % (h, u), b_banks[number], [P, 2, 2, P])
            for e, c, t in blocks(h, u):
                turn(gap_turned[h, u][:, e, c, :], wide[t][:, block(h, c)], e == 0 and c == 0, False)

        minus_a = [sb("minus_a%d" % t, [P, S], F32) for t in range(PACK)]
        minus_larger = [sb("minus_larger%d" % t, [P, S], F32) for t in range(PACK)]
        for t in range(PACK):
            a_bank = bank("a_bank%d" % t, a_banks[t], [P, S])
            product(nc, a_bank[:], w_words[W2], w_scales[W2], t, z_codes[:], z_scales[:])
            nc.vector.scalar_tensor_tensor(
                out=minus_larger[t][:], in0=b6[t][:], scalar=-1.0, in1=a_bank[:], op0=ALU.mult, op1=ALU.min
            )
            nc.scalar.copy(out=minus_a[t][:], in_=a_bank[:])

        staged = {}
        for h, u in quarters:
            for e, c, t in blocks(h, u):
                turn(gap_turned[h, u][:, e, c, :], minus_larger[t][:, block(h, c)], False, e == 1 and c == 1)
            staged[h, u] = sb("staged%d_%d" % (h, u), [P, 2, 2, P], F32)
            nc.scalar.copy(out=staged[h, u][:], in_=gap_turned[h, u][:])
        gap = {}
        for number, (h, u) in enumerate(sorted(quarters)):
            gap[h, u] = bank("gap%d_%d" % (h, u), a_banks[number], [P, 2, 2, P])
            for e, c, t in blocks(h, u):
                nc.tensor.transpose(gap[h, u][:, e, c, :], staged[h, u][:, e, c, :], identity[:])

        out_codes = sb("out_codes", [P, S], U32)
        out_scales = sb("out_scales", [P, S], U8)
        out_rows = out_0.rearrange("(p t) j -> p t j", t=PACK)
        out_words = out_1[0].rearrange("p n t -> p (n t)").bitcast(I32)
        excess = {}
        result = [sb("result%d" % h, [P, PACK, HALF], F32) for h in range(2)]

        def look_up(h, t, after=None):
            excess[h, t] = sb("excess%d_%d" % (h, t), [P, HALF], F32, after=after)
            nc.vector.tensor_tensor(excess[h, t][:], minus_a[t][:].indirect(entries("n5", h)), wide[t][:, cols(h)], ALU.add)

        def join(h, t):
            nc.vector.scalar_tensor_tensor(
                out=result[h][:, t, :],
                in0=excess[h, t][:],
                scalar=0.0,
                in1=gap[h, t // 2][:, t % 2, :, :].rearrange("p c j -> p (c j)"),
                op0=ALU.max,
                op1=ALU.subtract,
            )
            nc.sync.dma_start(out=out_rows[:, t, cols(h)], in_=result[h][:, t, :])

        def hand_on(h, copy):
            result_woven = sb("result_woven%d" % h, [P, PACK * HALF], BF16)
            weave(copy, result_woven[:], result[h][:])
            nc.vector.quantize_mx(out=out_codes[:, cols(h)].bitcast(FP8X4), scales=out_scales[:, cols(h)], in_=result_woven[:])
            nc.sync.dma_start(out=out_words[:, cols(h)], in_=out_codes[:, cols(h)].bitcast(I32))

        for t in range(PACK):
            look_up(0, t)
        look_up(1, 0)
        look_up(1, 1)
        join(0, 0)
        join(0, 1)
        look_up(1, 2, after="excess0_1")
        join(0, 2)
        join(0, 3)
        look_up(1, 3, after="excess0_3")
        hand_on(0, nc.scalar.copy)
        for t in range(PACK):
            join(1, t)
        hand_on(1, nc.vector.tensor_copy)

        for q in range(QUADRANTS):
            queue = nc.sync if q % 2 == 0 else nc.scalar
            queue.dma_start(out=out_2[0, 4 * q : 4 * q + 4, :].bitcast(I32), in_=out_scales[32 * q : 32 * q + 4, :].bitcast(I32))
